import numpy as np
import ml_dtypes


def mxq(x, axis, fmt="e4m3"):
    dtype, down = {"e4m3": (ml_dtypes.float8_e4m3fn, 7), "e5m2": (ml_dtypes.float8_e5m2, 14)}[fmt]
    v = np.moveaxis(np.asarray(x, np.float32).astype(ml_dtypes.bfloat16).astype(np.float64), axis, -1)
    blocks = v.reshape(v.shape[:-1] + (-1, 32))
    amax = np.abs(blocks).max(-1, keepdims=True)
    byte = np.maximum(np.where(amax > 0, np.frexp(amax)[1] - 1 + 127, 0) - down, 1)
    scale = np.exp2(byte - 127.0)
    codes = (blocks / scale).astype(np.float32).astype(dtype).astype(np.float64)
    return np.moveaxis((codes * scale).reshape(v.shape), -1, axis)


WIDE = False


def mx_kscale(k):
    if not WIDE:
        return np.ones(k)
    levels = np.array([10, -10, 5, -5, 0])
    if k % 512:
        return np.exp2(np.random.permutation(np.resize(levels, k // 32))).repeat(32)
    a = np.empty((k // 512, 16))
    for p in range(k // 512):
        a[p, :8] = np.random.permutation(np.resize(levels, 8))
        for g in range(8):
            far = levels[np.abs(levels - a[p, g]) >= 10]
            a[p, g + 8] = far[np.random.randint(len(far))]
    return np.exp2(a.ravel()).repeat(32)


def f64(x):
    return np.asarray(x).astype(np.float64)


def striped(idx):
    return np.tile(idx.reshape(-1, 16).T, (8, 1)).astype(np.uint16)


def unstriped(offs):
    return offs[:16].T.reshape(-1).astype(np.int64)


def pack_weight(w):
    k, n = w.shape
    w = f64(np.asarray(w, np.float32).astype(ml_dtypes.bfloat16)).reshape(k // 32, 32, n)
    amax = np.abs(w).max(1)
    byte = np.clip(np.where(amax > 0, np.frexp(amax)[1] - 1 + 127 - 7, 1), 1, 254)
    scaled = (w * np.exp2(127.0 - byte)[:, None, :]).reshape(k, n).astype(np.float32)
    words = np.ascontiguousarray(scaled.reshape(k // 512, 128, 4, n).transpose(0, 1, 3, 2)).astype(ml_dtypes.float8_e4m3fn).view(np.uint8)
    return words, np.ascontiguousarray(byte.astype(np.uint8).reshape(k // 512, 16, n))


def unpack_weight(words, scales):
    g, p, n, _ = words.shape
    vals = np.ascontiguousarray(words).view(ml_dtypes.float8_e4m3fn).astype(np.float64) * np.repeat(np.exp2(scales.astype(np.float64) - 127.0), 8, axis=1)[..., None]
    return vals.transpose(0, 1, 3, 2).reshape(g * 512, n)


K, T, S, H = 512, 2048, 512, 512


def setup_inputs():
    n = np.random.standard_normal
    s = mx_kscale(K)[:, None]
    u = mx_kscale(S)
    packed_xT = pack_weight(n((K, T)) * s)
    return {
        "x_words": packed_xT[0],
        "x_scales": packed_xT[1],
        "wa": (n((K, H)) / np.sqrt(K) / s).astype(np.float32),
        "wb": (n((K, H)) / np.sqrt(K) / s).astype(np.float32),
        "gt": (np.random.uniform(0.5, 1.5, (S, 1)) * u[:, None]).astype(np.float32),
        "gi": (np.random.uniform(0.5, 1.5, (S, 1)) / u[:, None]).astype(np.float32),
        "old": n((H, H)).astype(np.float32),
        "offs": striped(np.random.permutation(T)[:S]),
        "two": striped(np.random.permutation(T)[:S]),
    }


def reference(x_words, x_scales, wa, wb, gt, gi, old, offs, two):
    xq = unpack_weight(x_words, x_scales)[:, unstriped(offs)]
    a = xq.T @ mxq(f64(wa), 0, "e4m3")
    z = f64(gt) * a
    x_two = unpack_weight(x_words, x_scales)[:, unstriped(two)]
    b = x_two.T @ mxq(f64(wb), 0, "e4m3")
    z2 = f64(gi) * b
    cv = 0.0625 * ((mxq(z, 0, "e4m3").T @ mxq(z2, 0, "e4m3")))
    return f64(old) + 0.25 * (cv - f64(old))

@@ -1,0 +1,244 @@
+from contextlib import ExitStack
+
+import concourse.mybir as mybir
+
+K, T, S, H = 512, 2048, 512, 512
+FLOPS = 3 * 2 * 512 * 512 * 512
+
+F32 = mybir.dt.float32
+BF16 = mybir.dt.bfloat16
+I32 = mybir.dt.int32
+U32 = mybir.dt.uint32
+U16 = mybir.dt.uint16
+U8 = mybir.dt.uint8
+FP8X4 = mybir.dt.float8_e4m3fn_x4
+MULT = mybir.AluOpType.mult
+ADD = mybir.AluOpType.add
+COPY = mybir.ActivationFunctionType.Copy
+
+P = 128
+PACK = 4
+RUN = 8
+HALF = H // 2
+CH = 128
+SCALAR_CHUNKS = ()
+
+
+def tile_picked_crosscov_none_p_kernel(
+    tc, x_words, x_scales, wa, wb, gt, gi, old, offs, two, out
+):
+    nc = tc.nc
+    with ExitStack() as ctx:
+        keep = ctx.enter_context(tc.tile_pool(name="keep", bufs=1))
+        stage = ctx.enter_context(tc.tile_pool(name="stage", bufs=1))
+        proj = ctx.enter_context(tc.psum_pool(name="proj", bufs=4))
+        cvp = ctx.enter_context(tc.psum_pool(name="cvp", bufs=3))
+        gp = ctx.enter_context(tc.psum_pool(name="gp", bufs=1))
+
+        def sb(name, shape, dtype, tag=None):
+            return keep.tile(shape, dtype, name=name, tag=tag or name, align_bytes=64)
+
+        list_b = keep.tile([P, S // 16], U16, name="list_b")
+        list_a = keep.tile([P, S // 16], U16, name="list_a")
+        scale_win = sb("scale_win", [P, T], U8)
+        gate_rows = sb("gate_rows", [P, P], F32)
+        ident = sb("ident", [P, P], F32)
+        zeros = stage.tile([P, P], F32, name="zeros", offset=4 * T - 256)
+
+        nc.vector.memset(scale_win[:].bitcast(I32), 0)
+        nc.gpsimd.memset(zeros[:], 0.0)
+        nc.gpsimd.affine_select(
+            out=ident[:],
+            in_=zeros[:],
+            compare_op=mybir.AluOpType.not_equal,
+            fill=1.0,
+            base=0,
+            pattern=[[-1, P]],
+            channel_multiplier=1,
+        )
+        nc.gpsimd.memset(gate_rows[:], 0.0)
+        nc.sync.dma_start(list_b[:], two)
+        nc.sync.dma_start(list_a[:], offs)
+        raw = {}
+
+        def load_w(s, w, h, dst):
+            raw[s, h] = dst
+            nc.sync.dma_start(dst, w.rearrange("(p j) c -> p j c", j=PACK)[:, :, h * HALF : (h + 1) * HALF])
+
+        for q in range(4):
+            (nc.sync, nc.scalar)[q % 2].dma_start(
+                scale_win[32 * q : 32 * q + 4, :].bitcast(I32), x_scales[0, 4 * q : 4 * q + 4, :].bitcast(I32)
+            )
+        word_win = stage.tile([P, T], U32, name="word_win", offset=0)
+        later = stage.tile([P, 6, PACK, HALF], F32, name="later", offset=4 * T)
+        nc.sync.dma_start(word_win[:].bitcast(I32), x_words[0].rearrange("p n t -> p (n t)").bitcast(I32))
+        load_w("b", wb, 0, later[:, 5])
+        for i, g in enumerate((gt, gi)):
+            nc.sync.dma_start(
+                gate_rows[PACK * i : PACK * (i + 1), :].rearrange("t (b r) -> t b r", r=RUN),
+                g.rearrange("(b t r) o -> t b (r o)", t=PACK, r=RUN),
+            )
+        load_w("b", wb, 1, later[:, 0])
+        load_w("a", wa, 0, later[:, 1])
+        load_w("a", wa, 1, later[:, 2])
+        old_sb = [later[:, 3 + c // 2, 2 * (c % 2) : 2 * (c % 2) + 2, :].rearrange("p u n -> p (u n)") for c in range(4)]
+        for c in range(4):
+            nc.sync.dma_start(old_sb[c], old[c * P : (c + 1) * P, :])
+        gate_ps = gp.tile([P, P], F32, name="gate_ps")
+        nc.tensor.transpose(gate_ps[:], gate_rows[:], ident[:])
+        gates = sb("gates", [P, 2 * PACK], F32)
+        nc.scalar.activation(gates[:], gate_ps[:, 0 : 2 * PACK], COPY, scale=0.125)
+        gate = {"a": gates[:, 0:PACK], "b": gates[:, PACK : 2 * PACK]}
+
+        lists = {"a": list_a, "b": list_b}
+        picked_bytes, x_sc, x_cd = {}, {}, {}
+        for s in ("b", "a"):
+            picked_bytes[s] = sb("picked_bytes_" + s, [P, S], U8, "slot_x" + s)
+            nc.vector.tensor_copy(picked_bytes[s][:], scale_win[:].indirect(lists[s][:]))
+        for s in ("b", "a"):
+            x_sc[s] = sb("x_sc_" + s, [P, S], U8)
+            nc.vector.tensor_copy(
+                x_sc[s][:].bitcast(I32).rearrange("p (t b r) -> p t b r", t=PACK, r=RUN // 4),
+                picked_bytes[s][:].bitcast(I32).rearrange("p (b t r) -> p t b r", t=PACK, r=RUN // 4),
+            )
+        for s in ("b", "a"):
+            x_cd[s] = sb("x_cd_" + s, [P, S], U32, "slot_x" + {"a": "b", "b": "a"}[s])
+            nc.vector.tensor_copy(
+                x_cd[s][:].rearrange("p (t b r) -> p b t r", t=PACK, r=RUN), word_win[:].indirect(lists[s][:])
+            )
+
+        w_in, w_cd, w_sc = {}, {}, {}
+
+        def weave_w(s, h):
+            w_in[s, h] = sb("w_in_%s%d" % (s, h), [P, HALF, PACK], BF16)
+            nc.scalar.copy(
+                w_in[s, h][:].rearrange("p (c i) j -> p c j i", i=4),
+                raw[s, h].rearrange("p j (c i) -> p c j i", i=4),
+            )
+
+        def quant_w(s, h):
+            w_cd[s, h] = sb("w_cd_%s%d" % (s, h), [P, HALF], U32)
+            w_sc[s, h] = sb("w_sc_%s%d" % (s, h), [P, HALF], U8)
+            nc.vector.quantize_mx(
+                out=w_cd[s, h][:].bitcast(FP8X4), scales=w_sc[s, h][:], in_=w_in[s, h][:].rearrange("p c j -> p (c j)")
+            )
+
+        banks = {}
+
+        def project(s, c):
+            h, cols = c // 2, slice((c % 2) * CH, (c % 2 + 1) * CH)
+            banks[s, c] = proj.tile([P, PACK, CH], F32, name="proj_bank")
+            for t in range(PACK):
+                nc.tensor.matmul_mx(
+                    out=banks[s, c][:, t, :],
+                    lhsT=x_cd[s][:, t * P : (t + 1) * P].bitcast(FP8X4),
+                    lhsT_scale=x_sc[s][:, t * P : (t + 1) * P],
+                    rhs=w_cd[s, h][:, cols].bitcast(FP8X4),
+                    rhs_scale=w_sc[s, h][:, cols],
+                    start=True,
+                    stop=True,
+                )
+
+        def weigh_vector(s, c, dst):
+            nc.vector.tensor_tensor(
+                dst,
+                banks[s, c][:].rearrange("p t n -> p n t"),
+                gate[s].rearrange("p (o t) -> p o t", o=1).to_broadcast([P, CH, PACK]),
+                MULT,
+            )
+
+        pairs = {}
+
+        def weigh_scalar(s, c):
+            pairs[s, c] = sb("pairs_%s%d" % (s, c), [P, 2, CH, 2], BF16)
+            for t in range(PACK):
+                nc.scalar.activation(
+                    pairs[s, c][:, t // 2, :, t % 2], banks[s, c][:, t, :], COPY, scale=gate[s][:, t : t + 1]
+                )
+
+        def weave_pairs(s, c, dst):
+            nc.vector.tensor_copy(
+                dst.bitcast(F32),
+                pairs[s, c][:].rearrange("p u n e -> p u (n e)").bitcast(F32).rearrange("p u n -> p n u"),
+            )
+
+        z2_in = [sb("z2_in%d" % h, [P, HALF, PACK], BF16) for h in range(2)]
+        z2_cd = sb("z2_cd", [P, H], U32)
+        z2_sc = sb("z2_sc", [P, H], U8)
+
+        def quant_z2(h):
+            cols = slice(h * HALF, (h + 1) * HALF)
+            nc.vector.quantize_mx(
+                out=z2_cd[:, cols].bitcast(FP8X4), scales=z2_sc[:, cols], in_=z2_in[h][:].rearrange("p c j -> p (c j)")
+            )
+
+        def z2_dst(c):
+            return z2_in[c // 2][:, (c % 2) * CH : (c % 2 + 1) * CH, :]
+
+        weave_w("b", 0)
+        weave_w("b", 1)
+        weave_w("a", 0)
+        weave_w("a", 1)
+        quant_w("b", 0)
+        project("b", 0)
+        project("b", 1)
+        weigh_vector("b", 0, z2_dst(0))
+        quant_w("b", 1)
+        project("b", 2)
+        project("b", 3)
+        weigh_vector("b", 1, z2_dst(1))
+        weigh_vector("b", 2, z2_dst(2))
+        quant_z2(0)
+        quant_w("a", 0)
+        project("a", 0)
+        project("a", 1)
+        weigh_vector("b", 3, z2_dst(3))
+
+        z_in = [sb("z_in%d" % c, [P, CH, PACK], BF16) for c in range(4)]
+        z_cd = [sb("z_cd%d" % c, [P, CH], U32) for c in range(4)]
+        z_sc = [sb("z_sc%d" % c, [P, CH], U8) for c in range(4)]
+        cv = {}
+
+        def weigh_a(c):
+            if c in SCALAR_CHUNKS:
+                weigh_scalar("a", c)
+                weave_pairs("a", c, z_in[c][:])
+            else:
+                weigh_vector("a", c, z_in[c][:])
+
+        def moments(c):
+            nc.vector.quantize_mx(
+                out=z_cd[c][:].bitcast(FP8X4), scales=z_sc[c][:], in_=z_in[c][:].rearrange("p c j -> p (c j)")
+            )
+            cv[c] = cvp.tile([P, H], F32, name="cv_bank")
+            nc.tensor.matmul_mx(
+                out=cv[c][:],
+                lhsT=z_cd[c][:].bitcast(FP8X4),
+                lhsT_scale=z_sc[c][:],
+                rhs=z2_cd[:].bitcast(FP8X4),
+                rhs_scale=z2_sc[:],
+                start=True,
+                stop=True,
+            )
+
+        def finish(c):
+            res = sb("res%d" % c, [P, H], F32)
+            nc.vector.scalar_tensor_tensor(res[:], old_sb[c], 0.75, cv[c][:], MULT, ADD)
+            nc.sync.dma_start(out[c * P : (c + 1) * P, :], res[:])
+
+        weigh_a(0)
+        quant_z2(1)
+        quant_w("a", 1)
+        project("a", 2)
+        project("a", 3)
+        weigh_a(1)
+        moments(0)
+        weigh_a(2)
+        moments(1)
+        weigh_a(3)
+        moments(2)
+        finish(0)
+        moments(3)
+        finish(1)
+        finish(2)
+        finish(3)

@@ -21,7 +21,7 @@ PACK = 4
 RUN = 8
 HALF = H // 2
 CH = 128
-SCALAR_CHUNKS = ()
+PIECES = {"b": ((0, 128), (128, 128), (256, 256)), "a": ((0, 256), (256, 256))}
 
 
 def tile_picked_crosscov_none_p_kernel(
@@ -32,8 +32,7 @@ def tile_picked_crosscov_none_p_kernel(
         keep = ctx.enter_context(tc.tile_pool(name="keep", bufs=1))
         stage = ctx.enter_context(tc.tile_pool(name="stage", bufs=1))
         proj = ctx.enter_context(tc.psum_pool(name="proj", bufs=4))
-        cvp = ctx.enter_context(tc.psum_pool(name="cvp", bufs=3))
-        gp = ctx.enter_context(tc.psum_pool(name="gp", bufs=1))
+        cvp = ctx.enter_context(tc.psum_pool(name="cvp", bufs=4))
 
         def sb(name, shape, dtype, tag=None):
             return keep.tile(shape, dtype, name=name, tag=tag or name, align_bytes=64)
@@ -41,51 +40,54 @@ def tile_picked_crosscov_none_p_kernel(
         list_b = keep.tile([P, S // 16], U16, name="list_b")
         list_a = keep.tile([P, S // 16], U16, name="list_a")
         scale_win = sb("scale_win", [P, T], U8)
-        gate_rows = sb("gate_rows", [P, P], F32)
         ident = sb("ident", [P, P], F32)
-        zeros = stage.tile([P, P], F32, name="zeros", offset=4 * T - 256)
+        zeros = stage.tile([P, 4 * T + P], F32, name="zeros", offset=0)
 
         nc.vector.memset(scale_win[:].bitcast(I32), 0)
-        nc.gpsimd.memset(zeros[:], 0.0)
+        nc.gpsimd.memset(zeros[:, 0:P], 0.0)
         nc.gpsimd.affine_select(
             out=ident[:],
-            in_=zeros[:],
+            in_=zeros[:, 0:P],
             compare_op=mybir.AluOpType.not_equal,
             fill=1.0,
             base=0,
             pattern=[[-1, P]],
             channel_multiplier=1,
         )
+        gate_rows = stage.tile([P, P], F32, name="gate_rows", offset=4 * 4 * T)
         nc.gpsimd.memset(gate_rows[:], 0.0)
         nc.sync.dma_start(list_b[:], two)
         nc.sync.dma_start(list_a[:], offs)
         raw = {}
-
-        def load_w(s, w, h, dst):
-            raw[s, h] = dst
-            nc.sync.dma_start(dst, w.rearrange("(p j) c -> p j c", j=PACK)[:, :, h * HALF : (h + 1) * HALF])
 
         for q in range(4):
             (nc.sync, nc.scalar)[q % 2].dma_start(
                 scale_win[32 * q : 32 * q + 4, :].bitcast(I32), x_scales[0, 4 * q : 4 * q + 4, :].bitcast(I32)
             )
         word_win = stage.tile([P, T], U32, name="word_win", offset=0)
-        later = stage.tile([P, 6, PACK, HALF], F32, name="later", offset=4 * T)
+
+        def load_w(s, h):
+            c0, width = PIECES[s][h]
+            w, row = {"b": (wb, 1), "a": (wa, 2)}[s]
+            raw[s, h] = stage.tile([P, PACK, width], F32, name="raw_%s%d" % (s, h), offset=4 * (row * T + PACK * c0))
+            nc.sync.dma_start(raw[s, h][:], w.rearrange("(p j) c -> p j c", j=PACK)[:, :, c0 : c0 + width])
+
         nc.sync.dma_start(word_win[:].bitcast(I32), x_words[0].rearrange("p n t -> p (n t)").bitcast(I32))
-        load_w("b", wb, 0, later[:, 5])
+        load_w("b", 0)
         for i, g in enumerate((gt, gi)):
             nc.sync.dma_start(
                 gate_rows[PACK * i : PACK * (i + 1), :].rearrange("t (b r) -> t b r", r=RUN),
                 g.rearrange("(b t r) o -> t b (r o)", t=PACK, r=RUN),
             )
-        load_w("b", wb, 1, later[:, 0])
-        load_w("a", wa, 0, later[:, 1])
-        load_w("a", wa, 1, later[:, 2])
-        old_sb = [later[:, 3 + c // 2, 2 * (c % 2) : 2 * (c % 2) + 2, :].rearrange("p u n -> p (u n)") for c in range(4)]
+        load_w("b", 1)
+        load_w("b", 2)
+        load_w("a", 0)
+        load_w("a", 1)
+        old_sb = [stage.tile([P, H], F32, name="old%d" % c, offset=4 * (3 * T + c * H))[:] for c in range(4)]
         for c in range(4):
             nc.sync.dma_start(old_sb[c], old[c * P : (c + 1) * P, :])
-        gate_ps = gp.tile([P, P], F32, name="gate_ps")
-        nc.tensor.transpose(gate_ps[:], gate_rows[:], ident[:])
+        gate_ps = cvp.tile([P, H], F32, name="cv_bank")
+        nc.tensor.transpose(gate_ps[:, 0:P], gate_rows[:], ident[:])
         gates = sb("gates", [P, 2 * PACK], F32)
         nc.scalar.activation(gates[:], gate_ps[:, 0 : 2 * PACK], COPY, scale=0.125)
         gate = {"a": gates[:, 0:PACK], "b": gates[:, PACK : 2 * PACK]}
@@ -101,8 +103,9 @@ def tile_picked_crosscov_none_p_kernel(
                 x_sc[s][:].bitcast(I32).rearrange("p (t b r) -> p t b r", t=PACK, r=RUN // 4),
                 picked_bytes[s][:].bitcast(I32).rearrange("p (b t r) -> p t b r", t=PACK, r=RUN // 4),
             )
-        for s in ("b", "a"):
-            x_cd[s] = sb("x_cd_" + s, [P, S], U32, "slot_x" + {"a": "b", "b": "a"}[s])
+
+        def pick_words(s):
+            x_cd[s] = sb("x_cd_" + s, [P, S], U32, {"a": "slot_w", "b": "slot_xa"}[s])
             nc.vector.tensor_copy(
                 x_cd[s][:].rearrange("p (t b r) -> p b t r", t=PACK, r=RUN), word_win[:].indirect(lists[s][:])
             )
@@ -110,15 +113,15 @@ def tile_picked_crosscov_none_p_kernel(
         w_in, w_cd, w_sc = {}, {}, {}
 
         def weave_w(s, h):
-            w_in[s, h] = sb("w_in_%s%d" % (s, h), [P, HALF, PACK], BF16)
+            w_in[s, h] = sb("w_in_%s%d" % (s, h), [P, PIECES[s][h][1], PACK], BF16, {("b", 0): "slot_w", ("a", 0): "slot_z"}.get((s, h)))
             nc.scalar.copy(
                 w_in[s, h][:].rearrange("p (c i) j -> p c j i", i=4),
-                raw[s, h].rearrange("p j (c i) -> p c j i", i=4),
+                raw[s, h][:].rearrange("p j (c i) -> p c j i", i=4),
             )
 
         def quant_w(s, h):
-            w_cd[s, h] = sb("w_cd_%s%d" % (s, h), [P, HALF], U32)
-            w_sc[s, h] = sb("w_sc_%s%d" % (s, h), [P, HALF], U8)
+            w_cd[s, h] = sb("w_cd_%s%d" % (s, h), [P, PIECES[s][h][1]], U32)
+            w_sc[s, h] = sb("w_sc_%s%d" % (s, h), [P, PIECES[s][h][1]], U8)
             nc.vector.quantize_mx(
                 out=w_cd[s, h][:].bitcast(FP8X4), scales=w_sc[s, h][:], in_=w_in[s, h][:].rearrange("p c j -> p (c j)")
             )
@@ -126,7 +129,8 @@ def tile_picked_crosscov_none_p_kernel(
         banks = {}
 
         def project(s, c):
-            h, cols = c // 2, slice((c % 2) * CH, (c % 2 + 1) * CH)
+            h = max(i for i, (c0, width) in enumerate(PIECES[s]) if c0 <= c * CH)
+            cols = slice(c * CH - PIECES[s][h][0], (c + 1) * CH - PIECES[s][h][0])
             banks[s, c] = proj.tile([P, PACK, CH], F32, name="proj_bank")
             for t in range(PACK):
                 nc.tensor.matmul_mx(
@@ -147,22 +151,38 @@ def tile_picked_crosscov_none_p_kernel(
                 MULT,
             )
 
-        pairs = {}
+        pairs = sb("pairs", [P, 2, HALF, 2], BF16)
 
-        def weigh_scalar(s, c):
-            pairs[s, c] = sb("pairs_%s%d" % (s, c), [P, 2, CH, 2], BF16)
-            for t in range(PACK):
-                nc.scalar.activation(
-                    pairs[s, c][:, t // 2, :, t % 2], banks[s, c][:, t, :], COPY, scale=gate[s][:, t : t + 1]
-                )
+        def project_wide():
+            for u in range(2):
+                banks["wide", u] = proj.tile([P, 2, HALF], F32, name="proj_bank")
+                for e in range(2):
+                    t = 2 * u + e
+                    nc.tensor.matmul_mx(
+                        out=banks["wide", u][:, e, :],
+                        lhsT=x_cd["a"][:, t * P : (t + 1) * P].bitcast(FP8X4),
+                        lhsT_scale=x_sc["a"][:, t * P : (t + 1) * P],
+                        rhs=w_cd["a", 0][:].bitcast(FP8X4),
+                        rhs_scale=w_sc["a", 0][:],
+                        start=True,
+                        stop=True,
+                    )
 
-        def weave_pairs(s, c, dst):
+        def weigh_scalar():
+            for e in range(2):
+                for u in range(2):
+                    t = 2 * u + e
+                    nc.scalar.activation(
+                        pairs[:, u, :, e], banks["wide", u][:, e, :], COPY, scale=gate["a"][:, t : t + 1]
+                    )
+
+        def weave_pairs(dst):
             nc.vector.tensor_copy(
                 dst.bitcast(F32),
-                pairs[s, c][:].rearrange("p u n e -> p u (n e)").bitcast(F32).rearrange("p u n -> p n u"),
+                pairs[:].rearrange("p u n e -> p u (n e)").bitcast(F32).rearrange("p u n -> p n u"),
             )
 
-        z2_in = [sb("z2_in%d" % h, [P, HALF, PACK], BF16) for h in range(2)]
+        z2_in = {0: sb("z2_in0", [P, HALF, PACK], BF16)}
         z2_cd = sb("z2_cd", [P, H], U32)
         z2_sc = sb("z2_sc", [P, H], U8)
 
@@ -175,70 +195,76 @@ def tile_picked_crosscov_none_p_kernel(
         def z2_dst(c):
             return z2_in[c // 2][:, (c % 2) * CH : (c % 2 + 1) * CH, :]
 
-        weave_w("b", 0)
-        weave_w("b", 1)
-        weave_w("a", 0)
-        weave_w("a", 1)
+        for s in ("b", "a"):
+            for h in range(len(PIECES[s])):
+                weave_w(s, h)
         quant_w("b", 0)
+        pick_words("b")
         project("b", 0)
+        pick_words("a")
+        quant_w("b", 1)
         project("b", 1)
         weigh_vector("b", 0, z2_dst(0))
-        quant_w("b", 1)
+        quant_w("b", 2)
         project("b", 2)
         project("b", 3)
         weigh_vector("b", 1, z2_dst(1))
-        weigh_vector("b", 2, z2_dst(2))
         quant_z2(0)
         quant_w("a", 0)
-        project("a", 0)
-        project("a", 1)
+        project_wide()
+        z2_in[1] = sb("z2_in1", [P, HALF, PACK], BF16, "slot_z")
+        weigh_vector("b", 2, z2_dst(2))
+        quant_w("a", 1)
+        project("a", 2)
         weigh_vector("b", 3, z2_dst(3))
+        project("a", 3)
 
-        z_in = [sb("z_in%d" % c, [P, CH, PACK], BF16) for c in range(4)]
-        z_cd = [sb("z_cd%d" % c, [P, CH], U32) for c in range(4)]
-        z_sc = [sb("z_sc%d" % c, [P, CH], U8) for c in range(4)]
+        z_in = [sb("z_in%d" % h, [P, HALF, PACK], BF16) for h in range(2)]
+        z_cd = [sb("z_cd%d" % h, [P, HALF], U32) for h in range(2)]
+        z_sc = [sb("z_sc%d" % h, [P, HALF], U8) for h in range(2)]
         cv = {}
 
-        def weigh_a(c):
-            if c in SCALAR_CHUNKS:
-                weigh_scalar("a", c)
-                weave_pairs("a", c, z_in[c][:])
-            else:
-                weigh_vector("a", c, z_in[c][:])
+        def quant_z(h, cols):
+            nc.vector.quantize_mx(
+                out=z_cd[h][:, cols].bitcast(FP8X4),
+                scales=z_sc[h][:, cols],
+                in_=z_in[h][:, cols, :].rearrange("p c j -> p (c j)"),
+            )
 
         def moments(c):
-            nc.vector.quantize_mx(
-                out=z_cd[c][:].bitcast(FP8X4), scales=z_sc[c][:], in_=z_in[c][:].rearrange("p c j -> p (c j)")
-            )
+            h, cols = c // 2, slice((c % 2) * CH, (c % 2 + 1) * CH)
             cv[c] = cvp.tile([P, H], F32, name="cv_bank")
             nc.tensor.matmul_mx(
                 out=cv[c][:],
-                lhsT=z_cd[c][:].bitcast(FP8X4),
-                lhsT_scale=z_sc[c][:],
+                lhsT=z_cd[h][:, cols].bitcast(FP8X4),
+                lhsT_scale=z_sc[h][:, cols],
                 rhs=z2_cd[:].bitcast(FP8X4),
                 rhs_scale=z2_sc[:],
                 start=True,
                 stop=True,
             )
 
-        def finish(c):
-            res = sb("res%d" % c, [P, H], F32)
-            nc.vector.scalar_tensor_tensor(res[:], old_sb[c], 0.75, cv[c][:], MULT, ADD)
-            nc.sync.dma_start(out[c * P : (c + 1) * P, :], res[:])
+        def finish(c, pieces):
+            width = H // pieces
+            for i in range(pieces):
+                cols = slice(i * width, (i + 1) * width)
+                res = sb("res%d_%d" % (c, i), [P, width], F32)
+                nc.vector.scalar_tensor_tensor(res[:], old_sb[c][:, cols], 0.75, cv[c][:, cols], MULT, ADD)
+                nc.sync.dma_start(out[c * P : (c + 1) * P, cols], res[:])
 
-        weigh_a(0)
+        weigh_scalar()
+        weigh_vector("a", 2, z_in[1][:, 0:CH, :])
         quant_z2(1)
-        quant_w("a", 1)
-        project("a", 2)
-        project("a", 3)
-        weigh_a(1)
-        moments(0)
-        weigh_a(2)
-        moments(1)
-        weigh_a(3)
+        weigh_vector("a", 3, z_in[1][:, CH:HALF, :])
+        quant_z(1, slice(0, CH))
         moments(2)
-        finish(0)
+        quant_z(1, slice(CH, HALF))
         moments(3)
-        finish(1)
-        finish(2)
-        finish(3)
+        weave_pairs(z_in[0][:])
+        finish(2, 1)
+        quant_z(0, slice(0, HALF))
+        moments(0)
+        moments(1)
+        finish(3, 1)
+        finish(0, 1)
+        finish(1, 2)

@@ -21,7 +21,7 @@ PACK = 4
 RUN = 8
 HALF = H // 2
 CH = 128
-PIECES = {"b": ((0, 128), (128, 128), (256, 256)), "a": ((0, 256), (256, 256))}
+PIECES = {"b": ((0, 256), (256, 256)), "a": ((0, 256), (256, 256))}
 
 
 def tile_picked_crosscov_none_p_kernel(
@@ -40,8 +40,9 @@ def tile_picked_crosscov_none_p_kernel(
         list_b = keep.tile([P, S // 16], U16, name="list_b")
         list_a = keep.tile([P, S // 16], U16, name="list_a")
         scale_win = sb("scale_win", [P, T], U8)
+        word_win = sb("word_win", [P, T], U32)
         ident = sb("ident", [P, P], F32)
-        zeros = stage.tile([P, 4 * T + P], F32, name="zeros", offset=0)
+        zeros = stage.tile([P, 3 * T + P], F32, name="zeros", offset=0)
 
         nc.vector.memset(scale_win[:].bitcast(I32), 0)
         nc.gpsimd.memset(zeros[:, 0:P], 0.0)
@@ -54,25 +55,24 @@ def tile_picked_crosscov_none_p_kernel(
             pattern=[[-1, P]],
             channel_multiplier=1,
         )
-        gate_rows = stage.tile([P, P], F32, name="gate_rows", offset=4 * 4 * T)
+        gate_rows = stage.tile([P, P], F32, name="gate_rows", offset=4 * 3 * T)
         nc.gpsimd.memset(gate_rows[:], 0.0)
         nc.sync.dma_start(list_b[:], two)
+        nc.sync.dma_start(word_win[:].bitcast(I32), x_words[0].rearrange("p n t -> p (n t)").bitcast(I32))
         nc.sync.dma_start(list_a[:], offs)
         raw = {}
 
         for q in range(4):
-            (nc.sync, nc.scalar)[q % 2].dma_start(
+            nc.sync.dma_start(
                 scale_win[32 * q : 32 * q + 4, :].bitcast(I32), x_scales[0, 4 * q : 4 * q + 4, :].bitcast(I32)
             )
-        word_win = stage.tile([P, T], U32, name="word_win", offset=0)
 
         def load_w(s, h):
             c0, width = PIECES[s][h]
-            w, row = {"b": (wb, 1), "a": (wa, 2)}[s]
+            w, row = {"b": (wb, 0), "a": (wa, 1)}[s]
             raw[s, h] = stage.tile([P, PACK, width], F32, name="raw_%s%d" % (s, h), offset=4 * (row * T + PACK * c0))
             nc.sync.dma_start(raw[s, h][:], w.rearrange("(p j) c -> p j c", j=PACK)[:, :, c0 : c0 + width])
 
-        nc.sync.dma_start(word_win[:].bitcast(I32), x_words[0].rearrange("p n t -> p (n t)").bitcast(I32))
         load_w("b", 0)
         for i, g in enumerate((gt, gi)):
             nc.sync.dma_start(
@@ -80,10 +80,9 @@ def tile_picked_crosscov_none_p_kernel(
                 g.rearrange("(b t r) o -> t b (r o)", t=PACK, r=RUN),
             )
         load_w("b", 1)
-        load_w("b", 2)
         load_w("a", 0)
         load_w("a", 1)
-        old_sb = [stage.tile([P, H], F32, name="old%d" % c, offset=4 * (3 * T + c * H))[:] for c in range(4)]
+        old_sb = [stage.tile([P, H], F32, name="old%d" % c, offset=4 * (2 * T + c * H))[:] for c in range(4)]
         for c in range(4):
             nc.sync.dma_start(old_sb[c], old[c * P : (c + 1) * P, :])
         gate_ps = cvp.tile([P, H], F32, name="cv_bank")
@@ -94,10 +93,10 @@ def tile_picked_crosscov_none_p_kernel(
 
         lists = {"a": list_a, "b": list_b}
         picked_bytes, x_sc, x_cd = {}, {}, {}
-        for s in ("b", "a"):
-            picked_bytes[s] = sb("picked_bytes_" + s, [P, S], U8, "slot_x" + s)
+
+        def pick_scales(s):
+            picked_bytes[s] = sb("picked_bytes_" + s, [P, S], U8, {"a": "slot_w", "b": None}[s])
             nc.vector.tensor_copy(picked_bytes[s][:], scale_win[:].indirect(lists[s][:]))
-        for s in ("b", "a"):
             x_sc[s] = sb("x_sc_" + s, [P, S], U8)
             nc.vector.tensor_copy(
                 x_sc[s][:].bitcast(I32).rearrange("p (t b r) -> p t b r", t=PACK, r=RUN // 4),
@@ -105,7 +104,7 @@ def tile_picked_crosscov_none_p_kernel(
             )
 
         def pick_words(s):
-            x_cd[s] = sb("x_cd_" + s, [P, S], U32, {"a": "slot_w", "b": "slot_xa"}[s])
+            x_cd[s] = sb("x_cd_" + s, [P, S], U32)
             nc.vector.tensor_copy(
                 x_cd[s][:].rearrange("p (t b r) -> p b t r", t=PACK, r=RUN), word_win[:].indirect(lists[s][:])
             )
@@ -198,16 +197,17 @@ def tile_picked_crosscov_none_p_kernel(
         for s in ("b", "a"):
             for h in range(len(PIECES[s])):
                 weave_w(s, h)
-        quant_w("b", 0)
         pick_words("b")
-        project("b", 0)
         pick_words("a")
-        quant_w("b", 1)
+        pick_scales("b")
+        quant_w("b", 0)
+        project("b", 0)
         project("b", 1)
-        weigh_vector("b", 0, z2_dst(0))
-        quant_w("b", 2)
+        pick_scales("a")
+        quant_w("b", 1)
         project("b", 2)
         project("b", 3)
+        weigh_vector("b", 0, z2_dst(0))
         weigh_vector("b", 1, z2_dst(1))
         quant_z2(0)
         quant_w("a", 0)

@@ -113,10 +113,7 @@ def tile_picked_crosscov_none_p_kernel(
 
         def weave_w(s, h):
             w_in[s, h] = sb("w_in_%s%d" % (s, h), [P, PIECES[s][h][1], PACK], BF16, {("b", 0): "slot_w", ("a", 0): "slot_z"}.get((s, h)))
-            nc.scalar.copy(
-                w_in[s, h][:].rearrange("p (c i) j -> p c j i", i=4),
-                raw[s, h][:].rearrange("p j (c i) -> p c j i", i=4),
-            )
+            nc.scalar.copy(w_in[s, h][:], raw[s, h][:].rearrange("p j c -> p c j"))
 
         def quant_w(s, h):
             w_cd[s, h] = sb("w_cd_%s%d" % (s, h), [P, PIECES[s][h][1]], U32)

@@ -21,7 +21,8 @@ PACK = 4
 RUN = 8
 HALF = H // 2
 CH = 128
-PIECES = {"b": ((0, 256), (256, 256)), "a": ((0, 256), (256, 256))}
+LINE = 4
+RAW = 4 * PACK * HALF
 
 
 def tile_picked_crosscov_none_p_kernel(
@@ -31,18 +32,26 @@ def tile_picked_crosscov_none_p_kernel(
     with ExitStack() as ctx:
         keep = ctx.enter_context(tc.tile_pool(name="keep", bufs=1))
         stage = ctx.enter_context(tc.tile_pool(name="stage", bufs=1))
-        proj = ctx.enter_context(tc.psum_pool(name="proj", bufs=4))
-        cvp = ctx.enter_context(tc.psum_pool(name="cvp", bufs=4))
+        psum = ctx.enter_context(tc.psum_pool(name="psum", bufs=1))
 
-        def sb(name, shape, dtype, tag=None):
-            return keep.tile(shape, dtype, name=name, tag=tag or name, align_bytes=64)
+        def sb(name, shape, dtype):
+            return keep.tile(shape, dtype, name=name, align_bytes=64)
+
+        def staged(name, shape, dtype, offset):
+            return stage.tile(shape, dtype, name=name, offset=offset, align_bytes=64)
+
+        def bank(i, shape):
+            return psum.tile(shape, F32, name="bank", tag="bank%d" % i)
+
+        raw_at = {("b", 0): 0, ("b", 1): RAW, ("a", 0): 2 * RAW, ("a", 1): 3 * RAW}
+        old_at, gate_at = 4 * RAW, 6 * RAW
 
         list_b = keep.tile([P, S // 16], U16, name="list_b")
         list_a = keep.tile([P, S // 16], U16, name="list_a")
         scale_win = sb("scale_win", [P, T], U8)
         word_win = sb("word_win", [P, T], U32)
         ident = sb("ident", [P, P], F32)
-        zeros = stage.tile([P, 3 * T + P], F32, name="zeros", offset=0)
+        zeros = staged("zeros", [P, gate_at // 4 + P], F32, 0)
 
         nc.vector.memset(scale_win[:].bitcast(I32), 0)
         nc.gpsimd.memset(zeros[:, 0:P], 0.0)
@@ -55,53 +64,43 @@ def tile_picked_crosscov_none_p_kernel(
             pattern=[[-1, P]],
             channel_multiplier=1,
         )
-        gate_rows = stage.tile([P, P], F32, name="gate_rows", offset=4 * 3 * T)
+        gate_rows = staged("gate_rows", [P, P], F32, gate_at)
         nc.gpsimd.memset(gate_rows[:], 0.0)
         nc.sync.dma_start(list_b[:], two)
         nc.sync.dma_start(word_win[:].bitcast(I32), x_words[0].rearrange("p n t -> p (n t)").bitcast(I32))
         nc.sync.dma_start(list_a[:], offs)
-        raw = {}
-
         for q in range(4):
             nc.sync.dma_start(
                 scale_win[32 * q : 32 * q + 4, :].bitcast(I32), x_scales[0, 4 * q : 4 * q + 4, :].bitcast(I32)
             )
 
+        raw = {}
+
         def load_w(s, h):
-            c0, width = PIECES[s][h]
-            w, row = {"b": (wb, 0), "a": (wa, 1)}[s]
-            raw[s, h] = stage.tile([P, PACK, width], F32, name="raw_%s%d" % (s, h), offset=4 * (row * T + PACK * c0))
-            nc.sync.dma_start(raw[s, h][:], w.rearrange("(p j) c -> p j c", j=PACK)[:, :, c0 : c0 + width])
+            w = {"b": wb, "a": wa}[s]
+            raw[s, h] = staged("raw_%s%d" % (s, h), [P, PACK, HALF], F32, raw_at[s, h])
+            nc.sync.dma_start(raw[s, h][:], w.rearrange("(p j) c -> p j c", j=PACK)[:, :, h * HALF : (h + 1) * HALF])
 
         load_w("b", 0)
+        load_w("a", 0)
         for i, g in enumerate((gt, gi)):
             nc.sync.dma_start(
                 gate_rows[PACK * i : PACK * (i + 1), :].rearrange("t (b r) -> t b r", r=RUN),
                 g.rearrange("(b t r) o -> t b (r o)", t=PACK, r=RUN),
             )
         load_w("b", 1)
-        load_w("a", 0)
         load_w("a", 1)
-        old_sb = [stage.tile([P, H], F32, name="old%d" % c, offset=4 * (2 * T + c * H))[:] for c in range(4)]
+        old_sb = [staged("old%d" % c, [P, H], F32, old_at + 4 * c * H) for c in range(4)]
         for c in range(4):
-            nc.sync.dma_start(old_sb[c], old[c * P : (c + 1) * P, :])
-        gate_ps = cvp.tile([P, H], F32, name="cv_bank")
-        nc.tensor.transpose(gate_ps[:, 0:P], gate_rows[:], ident[:])
+            nc.sync.dma_start(old_sb[c][:], old[c * P : (c + 1) * P, :])
+        gate_ps = bank(7, [P, P])
+        nc.tensor.transpose(gate_ps[:], gate_rows[:], ident[:])
         gates = sb("gates", [P, 2 * PACK], F32)
         nc.scalar.activation(gates[:], gate_ps[:, 0 : 2 * PACK], COPY, scale=0.125)
         gate = {"a": gates[:, 0:PACK], "b": gates[:, PACK : 2 * PACK]}
 
         lists = {"a": list_a, "b": list_b}
-        picked_bytes, x_sc, x_cd = {}, {}, {}
-
-        def pick_scales(s):
-            picked_bytes[s] = sb("picked_bytes_" + s, [P, S], U8, {"a": "slot_w", "b": None}[s])
-            nc.vector.tensor_copy(picked_bytes[s][:], scale_win[:].indirect(lists[s][:]))
-            x_sc[s] = sb("x_sc_" + s, [P, S], U8)
-            nc.vector.tensor_copy(
-                x_sc[s][:].bitcast(I32).rearrange("p (t b r) -> p t b r", t=PACK, r=RUN // 4),
-                picked_bytes[s][:].bitcast(I32).rearrange("p (b t r) -> p t b r", t=PACK, r=RUN // 4),
-            )
+        picked, x_sc, x_cd = {}, {}, {}
 
         def pick_words(s):
             x_cd[s] = sb("x_cd_" + s, [P, S], U32)
@@ -109,35 +108,56 @@ def tile_picked_crosscov_none_p_kernel(
                 x_cd[s][:].rearrange("p (t b r) -> p b t r", t=PACK, r=RUN), word_win[:].indirect(lists[s][:])
             )
 
+        def pick_scales(s, dst):
+            picked[s] = dst
+            nc.vector.tensor_copy(dst[:], scale_win[:].indirect(lists[s][:]))
+
+        def deal_scales(s, dst):
+            x_sc[s] = dst
+            nc.vector.tensor_copy(
+                dst[:].bitcast(I32).rearrange("p (t b r) -> p t b r", t=PACK, r=RUN // 4),
+                picked[s][:].bitcast(I32).rearrange("p (b t r) -> p t b r", t=PACK, r=RUN // 4),
+            )
+
         w_in, w_cd, w_sc = {}, {}, {}
 
         def weave_w(s, h):
-            w_in[s, h] = sb("w_in_%s%d" % (s, h), [P, PIECES[s][h][1], PACK], BF16, {("b", 0): "slot_w", ("a", 0): "slot_z"}.get((s, h)))
-            nc.scalar.copy(w_in[s, h][:], raw[s, h][:].rearrange("p j c -> p c j"))
+            w_in[s, h] = sb("w_in_%s%d" % (s, h), [P, HALF, PACK], BF16)
+            nc.scalar.copy(
+                w_in[s, h][:].rearrange("p (c i) j -> p c j i", i=LINE),
+                raw[s, h][:].rearrange("p j (c i) -> p c j i", i=LINE),
+            )
 
         def quant_w(s, h):
-            w_cd[s, h] = sb("w_cd_%s%d" % (s, h), [P, PIECES[s][h][1]], U32)
-            w_sc[s, h] = sb("w_sc_%s%d" % (s, h), [P, PIECES[s][h][1]], U8)
+            w_cd[s, h] = sb("w_cd_%s%d" % (s, h), [P, HALF], U32)
+            w_sc[s, h] = sb("w_sc_%s%d" % (s, h), [P, HALF], U8)
             nc.vector.quantize_mx(
                 out=w_cd[s, h][:].bitcast(FP8X4), scales=w_sc[s, h][:], in_=w_in[s, h][:].rearrange("p c j -> p (c j)")
             )
 
         banks = {}
 
-        def project(s, c):
-            h = max(i for i, (c0, width) in enumerate(PIECES[s]) if c0 <= c * CH)
-            cols = slice(c * CH - PIECES[s][h][0], (c + 1) * CH - PIECES[s][h][0])
-            banks[s, c] = proj.tile([P, PACK, CH], F32, name="proj_bank")
+        def project(dst, s, t, h, cols):
+            nc.tensor.matmul_mx(
+                out=dst,
+                lhsT=x_cd[s][:, t * P : (t + 1) * P].bitcast(FP8X4),
+                lhsT_scale=x_sc[s][:, t * P : (t + 1) * P],
+                rhs=w_cd[s, h][:, cols].bitcast(FP8X4),
+                rhs_scale=w_sc[s, h][:, cols],
+                start=True,
+                stop=True,
+            )
+
+        def project_chunk(s, c, i):
+            banks[s, c] = bank(i, [P, PACK, CH])
             for t in range(PACK):
-                nc.tensor.matmul_mx(
-                    out=banks[s, c][:, t, :],
-                    lhsT=x_cd[s][:, t * P : (t + 1) * P].bitcast(FP8X4),
-                    lhsT_scale=x_sc[s][:, t * P : (t + 1) * P],
-                    rhs=w_cd[s, h][:, cols].bitcast(FP8X4),
-                    rhs_scale=w_sc[s, h][:, cols],
-                    start=True,
-                    stop=True,
-                )
+                project(banks[s, c][:, t, :], s, t, c // 2, slice((c % 2) * CH, (c % 2 + 1) * CH))
+
+        def project_wide():
+            for u in range(2):
+                banks["wide", u] = bank(4 + u, [P, 2, HALF])
+                for e in range(2):
+                    project(banks["wide", u][:, e, :], "a", 2 * u + e, 0, slice(0, HALF))
 
         def weigh_vector(s, c, dst):
             nc.vector.tensor_tensor(
@@ -147,90 +167,46 @@ def tile_picked_crosscov_none_p_kernel(
                 MULT,
             )
 
-        pairs = sb("pairs", [P, 2, HALF, 2], BF16)
+        def weigh_b(c):
+            weigh_vector("b", c, z2_in[:, c * CH : (c + 1) * CH, :])
 
-        def project_wide():
-            for u in range(2):
-                banks["wide", u] = proj.tile([P, 2, HALF], F32, name="proj_bank")
-                for e in range(2):
-                    t = 2 * u + e
-                    nc.tensor.matmul_mx(
-                        out=banks["wide", u][:, e, :],
-                        lhsT=x_cd["a"][:, t * P : (t + 1) * P].bitcast(FP8X4),
-                        lhsT_scale=x_sc["a"][:, t * P : (t + 1) * P],
-                        rhs=w_cd["a", 0][:].bitcast(FP8X4),
-                        rhs_scale=w_sc["a", 0][:],
-                        start=True,
-                        stop=True,
-                    )
+        pairs, z_in, z_cd, z_sc, cv = {}, {}, {}, {}, {}
 
-        def weigh_scalar():
+        def weigh_scalar(part, width, source):
+            pairs[part] = sb("pairs%d" % part, [P, 2, width, 2], BF16)
             for e in range(2):
                 for u in range(2):
                     t = 2 * u + e
-                    nc.scalar.activation(
-                        pairs[:, u, :, e], banks["wide", u][:, e, :], COPY, scale=gate["a"][:, t : t + 1]
-                    )
+                    nc.scalar.activation(pairs[part][:, u, :, e], source(u, e), COPY, scale=gate["a"][:, t : t + 1])
 
-        def weave_pairs(dst):
-            nc.vector.tensor_copy(
-                dst.bitcast(F32),
-                pairs[:].rearrange("p u n e -> p u (n e)").bitcast(F32).rearrange("p u n -> p n u"),
+        def weave_pairs(part, width, copy, word):
+            z_in[part] = sb("z_in%d" % part, [P, width, PACK], BF16)
+            copy(
+                z_in[part][:].bitcast(word),
+                pairs[part][:].rearrange("p u n e -> p u (n e)").bitcast(word).rearrange("p u n -> p n u"),
             )
 
-        z2_in = {0: sb("z2_in0", [P, HALF, PACK], BF16)}
         z2_cd = sb("z2_cd", [P, H], U32)
         z2_sc = sb("z2_sc", [P, H], U8)
 
         def quant_z2(h):
             cols = slice(h * HALF, (h + 1) * HALF)
             nc.vector.quantize_mx(
-                out=z2_cd[:, cols].bitcast(FP8X4), scales=z2_sc[:, cols], in_=z2_in[h][:].rearrange("p c j -> p (c j)")
+                out=z2_cd[:, cols].bitcast(FP8X4),
+                scales=z2_sc[:, cols],
+                in_=z2_in[:, cols, :].rearrange("p c j -> p (c j)"),
             )
 
-        def z2_dst(c):
-            return z2_in[c // 2][:, (c % 2) * CH : (c % 2 + 1) * CH, :]
-
-        for s in ("b", "a"):
-            for h in range(len(PIECES[s])):
-                weave_w(s, h)
-        pick_words("b")
-        pick_words("a")
-        pick_scales("b")
-        quant_w("b", 0)
-        project("b", 0)
-        project("b", 1)
-        pick_scales("a")
-        quant_w("b", 1)
-        project("b", 2)
-        project("b", 3)
-        weigh_vector("b", 0, z2_dst(0))
-        weigh_vector("b", 1, z2_dst(1))
-        quant_z2(0)
-        quant_w("a", 0)
-        project_wide()
-        z2_in[1] = sb("z2_in1", [P, HALF, PACK], BF16, "slot_z")
-        weigh_vector("b", 2, z2_dst(2))
-        quant_w("a", 1)
-        project("a", 2)
-        weigh_vector("b", 3, z2_dst(3))
-        project("a", 3)
-
-        z_in = [sb("z_in%d" % h, [P, HALF, PACK], BF16) for h in range(2)]
-        z_cd = [sb("z_cd%d" % h, [P, HALF], U32) for h in range(2)]
-        z_sc = [sb("z_sc%d" % h, [P, HALF], U8) for h in range(2)]
-        cv = {}
-
-        def quant_z(h, cols):
+        def quant_z(part, width):
+            z_cd[part] = keep.tile([P, width], U32, name="z_cd%d" % part, tag="z_cd%d" % (part % 3), align_bytes=64)
+            z_sc[part] = sb("z_sc%d" % part, [P, width], U8)
             nc.vector.quantize_mx(
-                out=z_cd[h][:, cols].bitcast(FP8X4),
-                scales=z_sc[h][:, cols],
-                in_=z_in[h][:, cols, :].rearrange("p c j -> p (c j)"),
+                out=z_cd[part][:].bitcast(FP8X4), scales=z_sc[part][:], in_=z_in[part][:].rearrange("p c j -> p (c j)")
             )
 
         def moments(c):
-            h, cols = c // 2, slice((c % 2) * CH, (c % 2 + 1) * CH)
-            cv[c] = cvp.tile([P, H], F32, name="cv_bank")
+            h, cols = (0, slice(c * CH, (c + 1) * CH)) if c < 2 else (c, slice(0, CH))
+            cv[c] = bank(c, [P, H])
             nc.tensor.matmul_mx(
                 out=cv[c][:],
                 lhsT=z_cd[h][:, cols].bitcast(FP8X4),
@@ -249,19 +225,47 @@ def tile_picked_crosscov_none_p_kernel(
                 nc.vector.scalar_tensor_tensor(res[:], old_sb[c][:, cols], 0.75, cv[c][:, cols], MULT, ADD)
                 nc.sync.dma_start(out[c * P : (c + 1) * P, cols], res[:])
 
-        weigh_scalar()
-        weigh_vector("a", 2, z_in[1][:, 0:CH, :])
+        for h in range(2):
+            for s in ("b", "a"):
+                weave_w(s, h)
+        pick_words("b")
+        pick_words("a")
+        pick_scales("b", sb("picked_b", [P, S], U8))
+        quant_w("b", 0)
+        deal_scales("b", staged("x_sc_b", [P, S], U8, raw_at["b", 0]))
+        pick_scales("a", staged("picked_a", [P, S], U8, raw_at["b", 0] + S))
+        project_chunk("b", 0, 0)
+        project_chunk("b", 1, 1)
+        quant_w("a", 0)
+        deal_scales("a", staged("x_sc_a", [P, S], U8, raw_at["a", 0]))
+        project_wide()
+        quant_w("b", 1)
+        project_chunk("b", 2, 2)
+        project_chunk("b", 3, 3)
+        z2_in = staged("z2_in", [P, H, PACK], BF16, raw_at["b", 1])
+        weigh_b(0)
+        weigh_scalar(0, HALF, lambda u, e: banks["wide", u][:, e, :])
+        weigh_b(1)
+        quant_w("a", 1)
+        project_chunk("a", 2, 6)
+        project_chunk("a", 3, 7)
+        weigh_scalar(2, CH, lambda u, e: banks["a", 2][:, 2 * u + e, :])
+        weigh_scalar(3, CH, lambda u, e: banks["a", 3][:, 2 * u + e, :])
+        weave_pairs(3, CH, nc.scalar.copy, U32)
+        weigh_b(2)
+        quant_z2(0)
+        weigh_b(3)
+        weave_pairs(0, HALF, nc.vector.tensor_copy, F32)
         quant_z2(1)
-        weigh_vector("a", 3, z_in[1][:, CH:HALF, :])
-        quant_z(1, slice(0, CH))
-        moments(2)
-        quant_z(1, slice(CH, HALF))
-        moments(3)
-        weave_pairs(z_in[0][:])
-        finish(2, 1)
-        quant_z(0, slice(0, HALF))
+        quant_z(0, HALF)
         moments(0)
         moments(1)
-        finish(3, 1)
+        weave_pairs(2, CH, nc.vector.tensor_copy, F32)
+        quant_z(2, CH)
+        moments(2)
         finish(0, 1)
-        finish(1, 2)
+        quant_z(3, CH)
+        moments(3)
+        finish(1, 1)
+        finish(2, 1)
+        finish(3, 2)

@@ -43,15 +43,87 @@ def tile_picked_crosscov_none_p_kernel(
         def bank(i, shape):
             return psum.tile(shape, F32, name="bank", tag="bank%d" % i)
 
-        raw_at = {("b", 0): 0, ("b", 1): RAW, ("a", 0): 2 * RAW, ("a", 1): 3 * RAW}
-        old_at, gate_at = 4 * RAW, 6 * RAW
+        def load_cols(dst, w, first, width):
+            nc.sync.dma_start(dst, w.rearrange("(p j) c -> p j c", j=PACK)[:, :, first : first + width])
+
+        def weave(copy, dst, src):
+            copy(dst.rearrange("p (c i) j -> p c j i", i=LINE), src.rearrange("p j (c i) -> p c j i", i=LINE))
+
+        def quantise(codes, scales, values):
+            nc.vector.quantize_mx(out=codes.bitcast(FP8X4), scales=scales, in_=values.rearrange("p c j -> p (c j)"))
+
+        def product(dst, lhs, lhs_sc, rhs, rhs_sc):
+            nc.tensor.matmul_mx(
+                out=dst, lhsT=lhs.bitcast(FP8X4), lhsT_scale=lhs_sc, rhs=rhs.bitcast(FP8X4), rhs_scale=rhs_sc,
+                start=True, stop=True,
+            )
+
+        def pick_words(dst, places):
+            nc.vector.tensor_copy(
+                dst[:].rearrange("p (t b r) -> p b t r", t=PACK, r=RUN), word_win[:].indirect(places[:])
+            )
+
+        def deal_scales(dst, src):
+            nc.vector.tensor_copy(
+                dst[:].bitcast(I32).rearrange("p (s t b r) -> p s t b r", s=2, t=PACK, r=RUN // 4),
+                src[:].bitcast(I32).rearrange("p (s b t r) -> p s t b r", s=2, t=PACK, r=RUN // 4),
+            )
+
+        def project_wide(first_bank, x_cd, x_sc, w_cd, w_sc):
+            banks = [bank(first_bank + u, [P, 2, HALF]) for u in range(2)]
+            for t in range(PACK):
+                rows = slice(t * P, (t + 1) * P)
+                product(banks[t // 2][:, t % 2, :], x_cd[:, rows], x_sc[:, rows], w_cd, w_sc)
+            return banks
+
+        def project_chunk(i, x_cd, x_sc, w_cd, w_sc):
+            dst = bank(i, [P, PACK, CH])
+            for t in range(PACK):
+                rows = slice(t * P, (t + 1) * P)
+                product(dst[:, t, :], x_cd[:, rows], x_sc[:, rows], w_cd, w_sc)
+            return dst
+
+        def weigh_vector(dst, src, gate):
+            nc.vector.tensor_tensor(
+                dst,
+                src[:].rearrange("p t n -> p n t"),
+                gate.rearrange("p (o t) -> p o t", o=1).to_broadcast([P, CH, PACK]),
+                MULT,
+            )
+
+        def weigh_scalar(pairs, banks, gate):
+            for t in range(PACK):
+                nc.scalar.activation(pairs[:, t // 2, :, t % 2], banks[t // 2][:, t % 2, :], COPY, scale=gate[:, t : t + 1])
+
+        def weigh_scalar_chunk(pairs, src, gate):
+            for t in range(PACK):
+                nc.scalar.activation(pairs[:, t // 2, :, t % 2], src[:, t, :], COPY, scale=gate[:, t : t + 1])
+
+        def join_pairs(copy, word, dst, pairs):
+            copy(
+                dst[:].bitcast(word),
+                pairs[:].rearrange("p u n e -> p u (n e)").bitcast(word).rearrange("p u n -> p n u"),
+            )
+
+        def finish(c, cv, pieces):
+            width = H // pieces
+            for i in range(pieces):
+                cols = slice(i * width, (i + 1) * width)
+                res = sb("res%d_%d" % (c, i), [P, width], F32)
+                nc.vector.scalar_tensor_tensor(res[:], old_sb[c][:, cols], 0.75, cv[:, cols], MULT, ADD)
+                nc.sync.dma_start(out[c * P : (c + 1) * P, cols], res[:])
+
+        QUART = RAW // 2
+        q0_at, word_at = 0, QUART
+        q1_at = word_at + 2 * RAW
+        a0_at = q1_at + QUART
+        b1_at, a1_at, old_at, gate_at = a0_at + RAW, a0_at + 2 * RAW, a0_at + 3 * RAW, a0_at + 5 * RAW
 
         list_b = keep.tile([P, S // 16], U16, name="list_b")
         list_a = keep.tile([P, S // 16], U16, name="list_a")
         scale_win = sb("scale_win", [P, T], U8)
-        word_win = sb("word_win", [P, T], U32)
         ident = sb("ident", [P, P], F32)
-        zeros = staged("zeros", [P, gate_at // 4 + P], F32, 0)
+        zeros = staged("zeros", [P, (gate_at - word_at) // 4 + P], F32, word_at)
 
         nc.vector.memset(scale_win[:].bitcast(I32), 0)
         nc.gpsimd.memset(zeros[:, 0:P], 0.0)
@@ -66,206 +138,122 @@ def tile_picked_crosscov_none_p_kernel(
         )
         gate_rows = staged("gate_rows", [P, P], F32, gate_at)
         nc.gpsimd.memset(gate_rows[:], 0.0)
+
         nc.sync.dma_start(list_b[:], two)
-        nc.sync.dma_start(word_win[:].bitcast(I32), x_words[0].rearrange("p n t -> p (n t)").bitcast(I32))
         nc.sync.dma_start(list_a[:], offs)
+        raw_q0 = staged("raw_q0", [P, PACK, CH], F32, q0_at)
+        load_cols(raw_q0[:], wb, 0, CH)
         for q in range(4):
             nc.sync.dma_start(
                 scale_win[32 * q : 32 * q + 4, :].bitcast(I32), x_scales[0, 4 * q : 4 * q + 4, :].bitcast(I32)
             )
-
-        raw = {}
-
-        def load_w(s, h):
-            w = {"b": wb, "a": wa}[s]
-            raw[s, h] = staged("raw_%s%d" % (s, h), [P, PACK, HALF], F32, raw_at[s, h])
-            nc.sync.dma_start(raw[s, h][:], w.rearrange("(p j) c -> p j c", j=PACK)[:, :, h * HALF : (h + 1) * HALF])
-
-        load_w("b", 0)
-        load_w("a", 0)
+        word_win = staged("word_win", [P, T], U32, word_at)
+        nc.sync.dma_start(word_win[:].bitcast(I32), x_words[0].rearrange("p n t -> p (n t)").bitcast(I32))
         for i, g in enumerate((gt, gi)):
             nc.sync.dma_start(
                 gate_rows[PACK * i : PACK * (i + 1), :].rearrange("t (b r) -> t b r", r=RUN),
                 g.rearrange("(b t r) o -> t b (r o)", t=PACK, r=RUN),
             )
-        load_w("b", 1)
-        load_w("a", 1)
+        raw_q1 = staged("raw_q1", [P, PACK, CH], F32, q1_at)
+        load_cols(raw_q1[:], wb, CH, CH)
+        raw_a0 = staged("raw_a0", [P, PACK, HALF], F32, a0_at)
+        load_cols(raw_a0[:], wa, 0, HALF)
+        raw_b1 = staged("raw_b1", [P, PACK, HALF], F32, b1_at)
+        load_cols(raw_b1[:], wb, HALF, HALF)
+        raw_a1 = staged("raw_a1", [P, PACK, HALF], F32, a1_at)
+        load_cols(raw_a1[:], wa, HALF, HALF)
         old_sb = [staged("old%d" % c, [P, H], F32, old_at + 4 * c * H) for c in range(4)]
         for c in range(4):
             nc.sync.dma_start(old_sb[c][:], old[c * P : (c + 1) * P, :])
+
         gate_ps = bank(7, [P, P])
         nc.tensor.transpose(gate_ps[:], gate_rows[:], ident[:])
-        gates = sb("gates", [P, 2 * PACK], F32)
+
+        w_q0 = sb("w_q0", [P, CH, PACK], BF16)
+        weave(nc.scalar.copy, w_q0[:], raw_q0[:])
+        w_q1 = sb("w_q1", [P, CH, PACK], BF16)
+        weave(nc.scalar.copy, w_q1[:], raw_q1[:])
+        w_a0 = sb("w_a0", [P, HALF, PACK], BF16)
+        weave(nc.scalar.copy, w_a0[:], raw_a0[:])
+        gates = staged("gates", [P, 2 * PACK], F32, a0_at)
         nc.scalar.activation(gates[:], gate_ps[:, 0 : 2 * PACK], COPY, scale=0.125)
-        gate = {"a": gates[:, 0:PACK], "b": gates[:, PACK : 2 * PACK]}
+        gate_a, gate_b = gates[:, 0:PACK], gates[:, PACK : 2 * PACK]
+        w_b1 = sb("w_b1", [P, HALF, PACK], BF16)
+        weave(nc.scalar.copy, w_b1[:], raw_b1[:])
+        w_a1 = sb("w_a1", [P, HALF, PACK], BF16)
+        weave(nc.scalar.copy, w_a1[:], raw_a1[:])
 
-        lists = {"a": list_a, "b": list_b}
-        picked, x_sc, x_cd = {}, {}, {}
+        picked = sb("picked", [P, 2 * S], U8)
+        nc.vector.tensor_copy(picked[:, 0:S], scale_win[:].indirect(list_b[:]))
+        nc.vector.tensor_copy(picked[:, S : 2 * S], scale_win[:].indirect(list_a[:]))
+        q0_cd, q0_sc = sb("q0_cd", [P, CH], U32), sb("q0_sc", [P, CH], U8)
+        quantise(q0_cd[:], q0_sc[:], w_q0[:])
+        x_sc = sb("x_sc", [P, 2 * S], U8)
+        deal_scales(x_sc, picked)
+        xb_sc, xa_sc = x_sc[:, 0:S], x_sc[:, S : 2 * S]
+        xb_cd = sb("xb_cd", [P, S], U32)
+        xa_cd = sb("xa_cd", [P, S], U32)
+        pick_words(xb_cd, list_b)
+        pick_words(xa_cd, list_a)
+        b0 = project_chunk(0, xb_cd, xb_sc, q0_cd[:], q0_sc[:])
+        q1_cd, q1_sc = sb("q1_cd", [P, CH], U32), sb("q1_sc", [P, CH], U8)
+        quantise(q1_cd[:], q1_sc[:], w_q1[:])
+        b1 = project_chunk(1, xb_cd, xb_sc, q1_cd[:], q1_sc[:])
+        a0_cd, a0_sc = sb("a0_cd", [P, HALF], U32), sb("a0_sc", [P, HALF], U8)
+        quantise(a0_cd[:], a0_sc[:], w_a0[:])
+        a01 = project_wide(4, xa_cd, xa_sc, a0_cd[:], a0_sc[:])
+        b1_cd, b1_sc = sb("b1_cd", [P, HALF], U32), sb("b1_sc", [P, HALF], U8)
+        quantise(b1_cd[:], b1_sc[:], w_b1[:])
+        b2 = project_chunk(2, xb_cd, xb_sc, b1_cd[:, 0:CH], b1_sc[:, 0:CH])
+        b3 = project_chunk(3, xb_cd, xb_sc, b1_cd[:, CH:HALF], b1_sc[:, CH:HALF])
+        a1_cd, a1_sc = sb("a1_cd", [P, HALF], U32), sb("a1_sc", [P, HALF], U8)
+        quantise(a1_cd[:], a1_sc[:], w_a1[:])
+        a2 = project_chunk(6, xa_cd, xa_sc, a1_cd[:, 0:CH], a1_sc[:, 0:CH])
+        a3 = project_chunk(7, xa_cd, xa_sc, a1_cd[:, CH:HALF], a1_sc[:, CH:HALF])
 
-        def pick_words(s):
-            x_cd[s] = sb("x_cd_" + s, [P, S], U32)
-            nc.vector.tensor_copy(
-                x_cd[s][:].rearrange("p (t b r) -> p b t r", t=PACK, r=RUN), word_win[:].indirect(lists[s][:])
-            )
+        pairs_a0 = staged("pairs_a0", [P, 2, HALF, 2], BF16, a1_at)
+        weigh_scalar(pairs_a0, a01, gate_a)
+        pairs_a2 = sb("pairs_a2", [P, 2, CH, 2], BF16)
+        weigh_scalar_chunk(pairs_a2, a2, gate_a)
+        pairs_a3 = sb("pairs_a3", [P, 2, CH, 2], BF16)
+        weigh_scalar_chunk(pairs_a3, a3, gate_a)
+        z_3 = sb("z_3", [P, CH, PACK], BF16)
+        join_pairs(nc.scalar.copy, U32, z_3, pairs_a3)
 
-        def pick_scales(s, dst):
-            picked[s] = dst
-            nc.vector.tensor_copy(dst[:], scale_win[:].indirect(lists[s][:]))
+        z2_0 = sb("z2_0", [P, CH, PACK], BF16)
+        z2_1 = staged("z2_1", [P, CH, PACK], BF16, b1_at)
+        z2_hi = sb("z2_hi", [P, HALF, PACK], BF16)
+        z2_cd, z2_sc = sb("z2_cd", [P, H], U32), staged("z2_sc", [P, H], U8, a1_at + RAW // 2)
+        weigh_vector(z2_0[:], b0, gate_b)
+        weigh_vector(z2_1[:], b1, gate_b)
+        quantise(z2_cd[:, 0:CH], z2_sc[:, 0:CH], z2_0[:])
+        quantise(z2_cd[:, CH:HALF], z2_sc[:, CH:HALF], z2_1[:])
+        weigh_vector(z2_hi[:, 0:CH, :], b2, gate_b)
+        weigh_vector(z2_hi[:, CH:HALF, :], b3, gate_b)
+        z_lo = sb("z_lo", [P, HALF, PACK], BF16)
+        join_pairs(nc.vector.tensor_copy, F32, z_lo, pairs_a0)
+        quantise(z2_cd[:, HALF:H], z2_sc[:, HALF:H], z2_hi[:])
+        cv = {}
 
-        def deal_scales(s, dst):
-            x_sc[s] = dst
-            nc.vector.tensor_copy(
-                dst[:].bitcast(I32).rearrange("p (t b r) -> p t b r", t=PACK, r=RUN // 4),
-                picked[s][:].bitcast(I32).rearrange("p (b t r) -> p t b r", t=PACK, r=RUN // 4),
-            )
+        def moments(c, i, codes, scales):
+            cv[c] = bank(i, [P, H])
+            product(cv[c][:], codes, scales, z2_cd[:], z2_sc[:])
 
-        w_in, w_cd, w_sc = {}, {}, {}
-
-        def weave_w(s, h):
-            w_in[s, h] = sb("w_in_%s%d" % (s, h), [P, HALF, PACK], BF16)
-            nc.scalar.copy(
-                w_in[s, h][:].rearrange("p (c i) j -> p c j i", i=LINE),
-                raw[s, h][:].rearrange("p j (c i) -> p c j i", i=LINE),
-            )
-
-        def quant_w(s, h):
-            w_cd[s, h] = sb("w_cd_%s%d" % (s, h), [P, HALF], U32)
-            w_sc[s, h] = sb("w_sc_%s%d" % (s, h), [P, HALF], U8)
-            nc.vector.quantize_mx(
-                out=w_cd[s, h][:].bitcast(FP8X4), scales=w_sc[s, h][:], in_=w_in[s, h][:].rearrange("p c j -> p (c j)")
-            )
-
-        banks = {}
-
-        def project(dst, s, t, h, cols):
-            nc.tensor.matmul_mx(
-                out=dst,
-                lhsT=x_cd[s][:, t * P : (t + 1) * P].bitcast(FP8X4),
-                lhsT_scale=x_sc[s][:, t * P : (t + 1) * P],
-                rhs=w_cd[s, h][:, cols].bitcast(FP8X4),
-                rhs_scale=w_sc[s, h][:, cols],
-                start=True,
-                stop=True,
-            )
-
-        def project_chunk(s, c, i):
-            banks[s, c] = bank(i, [P, PACK, CH])
-            for t in range(PACK):
-                project(banks[s, c][:, t, :], s, t, c // 2, slice((c % 2) * CH, (c % 2 + 1) * CH))
-
-        def project_wide():
-            for u in range(2):
-                banks["wide", u] = bank(4 + u, [P, 2, HALF])
-                for e in range(2):
-                    project(banks["wide", u][:, e, :], "a", 2 * u + e, 0, slice(0, HALF))
-
-        def weigh_vector(s, c, dst):
-            nc.vector.tensor_tensor(
-                dst,
-                banks[s, c][:].rearrange("p t n -> p n t"),
-                gate[s].rearrange("p (o t) -> p o t", o=1).to_broadcast([P, CH, PACK]),
-                MULT,
-            )
-
-        def weigh_b(c):
-            weigh_vector("b", c, z2_in[:, c * CH : (c + 1) * CH, :])
-
-        pairs, z_in, z_cd, z_sc, cv = {}, {}, {}, {}, {}
-
-        def weigh_scalar(part, width, source):
-            pairs[part] = sb("pairs%d" % part, [P, 2, width, 2], BF16)
-            for e in range(2):
-                for u in range(2):
-                    t = 2 * u + e
-                    nc.scalar.activation(pairs[part][:, u, :, e], source(u, e), COPY, scale=gate["a"][:, t : t + 1])
-
-        def weave_pairs(part, width, copy, word):
-            z_in[part] = sb("z_in%d" % part, [P, width, PACK], BF16)
-            copy(
-                z_in[part][:].bitcast(word),
-                pairs[part][:].rearrange("p u n e -> p u (n e)").bitcast(word).rearrange("p u n -> p n u"),
-            )
-
-        z2_cd = sb("z2_cd", [P, H], U32)
-        z2_sc = sb("z2_sc", [P, H], U8)
-
-        def quant_z2(h):
-            cols = slice(h * HALF, (h + 1) * HALF)
-            nc.vector.quantize_mx(
-                out=z2_cd[:, cols].bitcast(FP8X4),
-                scales=z2_sc[:, cols],
-                in_=z2_in[:, cols, :].rearrange("p c j -> p (c j)"),
-            )
-
-        def quant_z(part, width):
-            z_cd[part] = keep.tile([P, width], U32, name="z_cd%d" % part, tag="z_cd%d" % (part % 3), align_bytes=64)
-            z_sc[part] = sb("z_sc%d" % part, [P, width], U8)
-            nc.vector.quantize_mx(
-                out=z_cd[part][:].bitcast(FP8X4), scales=z_sc[part][:], in_=z_in[part][:].rearrange("p c j -> p (c j)")
-            )
-
-        def moments(c):
-            h, cols = (0, slice(c * CH, (c + 1) * CH)) if c < 2 else (c, slice(0, CH))
-            cv[c] = bank(c, [P, H])
-            nc.tensor.matmul_mx(
-                out=cv[c][:],
-                lhsT=z_cd[h][:, cols].bitcast(FP8X4),
-                lhsT_scale=z_sc[h][:, cols],
-                rhs=z2_cd[:].bitcast(FP8X4),
-                rhs_scale=z2_sc[:],
-                start=True,
-                stop=True,
-            )
-
-        def finish(c, pieces):
-            width = H // pieces
-            for i in range(pieces):
-                cols = slice(i * width, (i + 1) * width)
-                res = sb("res%d_%d" % (c, i), [P, width], F32)
-                nc.vector.scalar_tensor_tensor(res[:], old_sb[c][:, cols], 0.75, cv[c][:, cols], MULT, ADD)
-                nc.sync.dma_start(out[c * P : (c + 1) * P, cols], res[:])
-
-        for h in range(2):
-            for s in ("b", "a"):
-                weave_w(s, h)
-        pick_words("b")
-        pick_words("a")
-        pick_scales("b", sb("picked_b", [P, S], U8))
-        quant_w("b", 0)
-        deal_scales("b", staged("x_sc_b", [P, S], U8, raw_at["b", 0]))
-        pick_scales("a", staged("picked_a", [P, S], U8, raw_at["b", 0] + S))
-        project_chunk("b", 0, 0)
-        project_chunk("b", 1, 1)
-        quant_w("a", 0)
-        deal_scales("a", staged("x_sc_a", [P, S], U8, raw_at["a", 0]))
-        project_wide()
-        quant_w("b", 1)
-        project_chunk("b", 2, 2)
-        project_chunk("b", 3, 3)
-        z2_in = staged("z2_in", [P, H, PACK], BF16, raw_at["b", 1])
-        weigh_b(0)
-        weigh_scalar(0, HALF, lambda u, e: banks["wide", u][:, e, :])
-        weigh_b(1)
-        quant_w("a", 1)
-        project_chunk("a", 2, 6)
-        project_chunk("a", 3, 7)
-        weigh_scalar(2, CH, lambda u, e: banks["a", 2][:, 2 * u + e, :])
-        weigh_scalar(3, CH, lambda u, e: banks["a", 3][:, 2 * u + e, :])
-        weave_pairs(3, CH, nc.scalar.copy, U32)
-        weigh_b(2)
-        quant_z2(0)
-        weigh_b(3)
-        weave_pairs(0, HALF, nc.vector.tensor_copy, F32)
-        quant_z2(1)
-        quant_z(0, HALF)
-        moments(0)
-        moments(1)
-        weave_pairs(2, CH, nc.vector.tensor_copy, F32)
-        quant_z(2, CH)
-        moments(2)
-        finish(0, 1)
-        quant_z(3, CH)
-        moments(3)
-        finish(1, 1)
-        finish(2, 1)
-        finish(3, 2)
+        zlo_cd = keep.tile([P, HALF], U32, name="zlo_cd", tag="z_cd", align_bytes=64)
+        zlo_sc = sb("zlo_sc", [P, HALF], U8)
+        quantise(zlo_cd[:], zlo_sc[:], z_lo[:])
+        moments(0, 0, zlo_cd[:, 0:CH], zlo_sc[:, 0:CH])
+        moments(1, 1, zlo_cd[:, CH:HALF], zlo_sc[:, CH:HALF])
+        z_2 = sb("z_2", [P, CH, PACK], BF16)
+        join_pairs(nc.vector.tensor_copy, F32, z_2, pairs_a2)
+        z2c_cd, z2c_sc = sb("z2c_cd", [P, CH], U32), sb("z2c_sc", [P, CH], U8)
+        quantise(z2c_cd[:], z2c_sc[:], z_2[:])
+        moments(2, 2, z2c_cd[:], z2c_sc[:])
+        finish(0, cv[0], 1)
+        z3_cd = keep.tile([P, CH], U32, name="z3_cd", tag="z_cd", align_bytes=64)
+        z3_sc = sb("z3_sc", [P, CH], U8)
+        quantise(z3_cd[:], z3_sc[:], z_3[:])
+        moments(3, 3, z3_cd[:], z3_sc[:])
+        finish(1, cv[1], 1)
+        finish(2, cv[2], 1)
+        finish(3, cv[3], 2)

@@ -63,18 +63,10 @@ def tile_picked_crosscov_none_p_kernel(
                 dst[:].rearrange("p (t b r) -> p b t r", t=PACK, r=RUN), word_win[:].indirect(places[:])
             )
 
-        def deal_scales(dst, src):
+        def pick_scales(dst, places):
             nc.vector.tensor_copy(
-                dst[:].bitcast(I32).rearrange("p (s t b r) -> p s t b r", s=2, t=PACK, r=RUN // 4),
-                src[:].bitcast(I32).rearrange("p (s b t r) -> p s t b r", s=2, t=PACK, r=RUN // 4),
+                dst[:].rearrange("p (t b r) -> p b t r", t=PACK, r=RUN), scale_win[:].indirect(places[:])
             )
-
-        def project_wide(first_bank, x_cd, x_sc, w_cd, w_sc):
-            banks = [bank(first_bank + u, [P, 2, HALF]) for u in range(2)]
-            for t in range(PACK):
-                rows = slice(t * P, (t + 1) * P)
-                product(banks[t // 2][:, t % 2, :], x_cd[:, rows], x_sc[:, rows], w_cd, w_sc)
-            return banks
 
         def project_chunk(i, x_cd, x_sc, w_cd, w_sc):
             dst = bank(i, [P, PACK, CH])
@@ -91,17 +83,13 @@ def tile_picked_crosscov_none_p_kernel(
                 MULT,
             )
 
-        def weigh_scalar(pairs, banks, gate):
-            for t in range(PACK):
-                nc.scalar.activation(pairs[:, t // 2, :, t % 2], banks[t // 2][:, t % 2, :], COPY, scale=gate[:, t : t + 1])
-
         def weigh_scalar_chunk(pairs, src, gate):
             for t in range(PACK):
                 nc.scalar.activation(pairs[:, t // 2, :, t % 2], src[:, t, :], COPY, scale=gate[:, t : t + 1])
 
         def join_pairs(copy, word, dst, pairs):
             copy(
-                dst[:].bitcast(word),
+                dst.bitcast(word),
                 pairs[:].rearrange("p u n e -> p u (n e)").bitcast(word).rearrange("p u n -> p n u"),
             )
 
@@ -118,6 +106,8 @@ def tile_picked_crosscov_none_p_kernel(
         q1_at = word_at + 2 * RAW
         a0_at = q1_at + QUART
         b1_at, a1_at, old_at, gate_at = a0_at + RAW, a0_at + 2 * RAW, a0_at + 3 * RAW, a0_at + 5 * RAW
+
+        woven_at = gate_at + 4 * P
 
         list_b = keep.tile([P, S // 16], U16, name="list_b")
         list_a = keep.tile([P, S // 16], U16, name="list_a")
@@ -166,72 +156,73 @@ def tile_picked_crosscov_none_p_kernel(
         for c in range(4):
             nc.sync.dma_start(old_sb[c][:], old[c * P : (c + 1) * P, :])
 
-        gate_ps = bank(7, [P, P])
+        gate_ps = bank(0, [P, P])
         nc.tensor.transpose(gate_ps[:], gate_rows[:], ident[:])
 
         w_q0 = sb("w_q0", [P, CH, PACK], BF16)
         weave(nc.scalar.copy, w_q0[:], raw_q0[:])
+        gates = sb("gates", [P, 2 * PACK], F32)
+        nc.scalar.activation(gates[:], gate_ps[:, 0 : 2 * PACK], COPY, scale=0.125)
+        gate_a, gate_b = gates[:, 0:PACK], gates[:, PACK : 2 * PACK]
         w_q1 = sb("w_q1", [P, CH, PACK], BF16)
         weave(nc.scalar.copy, w_q1[:], raw_q1[:])
         w_a0 = sb("w_a0", [P, HALF, PACK], BF16)
         weave(nc.scalar.copy, w_a0[:], raw_a0[:])
-        gates = staged("gates", [P, 2 * PACK], F32, a0_at)
-        nc.scalar.activation(gates[:], gate_ps[:, 0 : 2 * PACK], COPY, scale=0.125)
-        gate_a, gate_b = gates[:, 0:PACK], gates[:, PACK : 2 * PACK]
-        w_b1 = sb("w_b1", [P, HALF, PACK], BF16)
+        w_b1 = staged("w_b1", [P, HALF, PACK], BF16, woven_at)
         weave(nc.scalar.copy, w_b1[:], raw_b1[:])
         w_a1 = sb("w_a1", [P, HALF, PACK], BF16)
         weave(nc.scalar.copy, w_a1[:], raw_a1[:])
 
-        picked = sb("picked", [P, 2 * S], U8)
-        nc.vector.tensor_copy(picked[:, 0:S], scale_win[:].indirect(list_b[:]))
-        nc.vector.tensor_copy(picked[:, S : 2 * S], scale_win[:].indirect(list_a[:]))
+        xb_sc = sb("xb_sc", [P, S], U8)
+        xa_sc = sb("xa_sc", [P, S], U8)
+        pick_scales(xb_sc, list_b)
+        pick_scales(xa_sc, list_a)
         q0_cd, q0_sc = sb("q0_cd", [P, CH], U32), sb("q0_sc", [P, CH], U8)
         quantise(q0_cd[:], q0_sc[:], w_q0[:])
-        x_sc = sb("x_sc", [P, 2 * S], U8)
-        deal_scales(x_sc, picked)
-        xb_sc, xa_sc = x_sc[:, 0:S], x_sc[:, S : 2 * S]
         xb_cd = sb("xb_cd", [P, S], U32)
         xa_cd = sb("xa_cd", [P, S], U32)
         pick_words(xb_cd, list_b)
         pick_words(xa_cd, list_a)
+        z2_0 = staged("z2_0", [P, CH, PACK], BF16, q1_at)
+        z2_1 = staged("z2_1", [P, CH, PACK], BF16, a0_at)
+        z_lo = staged("z_lo", [P, HALF, PACK], BF16, b1_at)
+        z2_hi = staged("z2_hi", [P, HALF, PACK], BF16, a1_at)
+        z2_cd, z2_sc = sb("z2_cd", [P, H], U32), staged("z2_sc", [P, H], U8, b1_at + RAW // 2)
+
         b0 = project_chunk(0, xb_cd, xb_sc, q0_cd[:], q0_sc[:])
         q1_cd, q1_sc = sb("q1_cd", [P, CH], U32), sb("q1_sc", [P, CH], U8)
         quantise(q1_cd[:], q1_sc[:], w_q1[:])
         b1 = project_chunk(1, xb_cd, xb_sc, q1_cd[:], q1_sc[:])
+        weigh_vector(z2_0[:], b0, gate_b)
         a0_cd, a0_sc = sb("a0_cd", [P, HALF], U32), sb("a0_sc", [P, HALF], U8)
         quantise(a0_cd[:], a0_sc[:], w_a0[:])
-        a01 = project_wide(4, xa_cd, xa_sc, a0_cd[:], a0_sc[:])
+        a0 = project_chunk(4, xa_cd, xa_sc, a0_cd[:, 0:CH], a0_sc[:, 0:CH])
+        a1 = project_chunk(5, xa_cd, xa_sc, a0_cd[:, CH:HALF], a0_sc[:, CH:HALF])
+        weigh_vector(z2_1[:], b1, gate_b)
         b1_cd, b1_sc = sb("b1_cd", [P, HALF], U32), sb("b1_sc", [P, HALF], U8)
         quantise(b1_cd[:], b1_sc[:], w_b1[:])
         b2 = project_chunk(2, xb_cd, xb_sc, b1_cd[:, 0:CH], b1_sc[:, 0:CH])
         b3 = project_chunk(3, xb_cd, xb_sc, b1_cd[:, CH:HALF], b1_sc[:, CH:HALF])
+        weigh_vector(z_lo[:, 0:CH, :], a0, gate_a)
+        quantise(z2_cd[:, 0:CH], z2_sc[:, 0:CH], z2_0[:])
+        quantise(z2_cd[:, CH:HALF], z2_sc[:, CH:HALF], z2_1[:])
         a1_cd, a1_sc = sb("a1_cd", [P, HALF], U32), sb("a1_sc", [P, HALF], U8)
         quantise(a1_cd[:], a1_sc[:], w_a1[:])
         a2 = project_chunk(6, xa_cd, xa_sc, a1_cd[:, 0:CH], a1_sc[:, 0:CH])
         a3 = project_chunk(7, xa_cd, xa_sc, a1_cd[:, CH:HALF], a1_sc[:, CH:HALF])
 
-        pairs_a0 = staged("pairs_a0", [P, 2, HALF, 2], BF16, a1_at)
-        weigh_scalar(pairs_a0, a01, gate_a)
+        pairs_a1 = staged("pairs_a1", [P, 2, CH, 2], BF16, woven_at)
+        weigh_scalar_chunk(pairs_a1, a1, gate_a)
         pairs_a2 = sb("pairs_a2", [P, 2, CH, 2], BF16)
         weigh_scalar_chunk(pairs_a2, a2, gate_a)
         pairs_a3 = sb("pairs_a3", [P, 2, CH, 2], BF16)
         weigh_scalar_chunk(pairs_a3, a3, gate_a)
         z_3 = sb("z_3", [P, CH, PACK], BF16)
-        join_pairs(nc.scalar.copy, U32, z_3, pairs_a3)
+        join_pairs(nc.scalar.copy, U32, z_3[:], pairs_a3)
 
-        z2_0 = sb("z2_0", [P, CH, PACK], BF16)
-        z2_1 = staged("z2_1", [P, CH, PACK], BF16, b1_at)
-        z2_hi = sb("z2_hi", [P, HALF, PACK], BF16)
-        z2_cd, z2_sc = sb("z2_cd", [P, H], U32), staged("z2_sc", [P, H], U8, a1_at + RAW // 2)
-        weigh_vector(z2_0[:], b0, gate_b)
-        weigh_vector(z2_1[:], b1, gate_b)
-        quantise(z2_cd[:, 0:CH], z2_sc[:, 0:CH], z2_0[:])
-        quantise(z2_cd[:, CH:HALF], z2_sc[:, CH:HALF], z2_1[:])
         weigh_vector(z2_hi[:, 0:CH, :], b2, gate_b)
         weigh_vector(z2_hi[:, CH:HALF, :], b3, gate_b)
-        z_lo = sb("z_lo", [P, HALF, PACK], BF16)
-        join_pairs(nc.vector.tensor_copy, F32, z_lo, pairs_a0)
+        join_pairs(nc.vector.tensor_copy, F32, z_lo[:, CH:HALF, :], pairs_a1)
         quantise(z2_cd[:, HALF:H], z2_sc[:, HALF:H], z2_hi[:])
         cv = {}
 
@@ -245,7 +236,7 @@ def tile_picked_crosscov_none_p_kernel(
         moments(0, 0, zlo_cd[:, 0:CH], zlo_sc[:, 0:CH])
         moments(1, 1, zlo_cd[:, CH:HALF], zlo_sc[:, CH:HALF])
         z_2 = sb("z_2", [P, CH, PACK], BF16)
-        join_pairs(nc.vector.tensor_copy, F32, z_2, pairs_a2)
+        join_pairs(nc.vector.tensor_copy, F32, z_2[:], pairs_a2)
         z2c_cd, z2c_sc = sb("z2c_cd", [P, CH], U32), sb("z2c_sc", [P, CH], U8)
         quantise(z2c_cd[:], z2c_sc[:], z_2[:])
         moments(2, 2, z2c_cd[:], z2c_sc[:])

@@ -63,9 +63,10 @@ def tile_picked_crosscov_none_p_kernel(
                 dst[:].rearrange("p (t b r) -> p b t r", t=PACK, r=RUN), word_win[:].indirect(places[:])
             )
 
-        def pick_scales(dst, places):
+        def deal_scales(dst, src):
             nc.vector.tensor_copy(
-                dst[:].rearrange("p (t b r) -> p b t r", t=PACK, r=RUN), scale_win[:].indirect(places[:])
+                dst[:].bitcast(I32).rearrange("p (t b r) -> p t b r", t=PACK, r=RUN // 4),
+                src[:].bitcast(I32).rearrange("p (b t r) -> p t b r", t=PACK, r=RUN // 4),
             )
 
         def project_chunk(i, x_cd, x_sc, w_cd, w_sc):
@@ -129,10 +130,10 @@ def tile_picked_crosscov_none_p_kernel(
         gate_rows = staged("gate_rows", [P, P], F32, gate_at)
         nc.gpsimd.memset(gate_rows[:], 0.0)
 
-        nc.sync.dma_start(list_b[:], two)
-        nc.sync.dma_start(list_a[:], offs)
         raw_q0 = staged("raw_q0", [P, PACK, CH], F32, q0_at)
         load_cols(raw_q0[:], wb, 0, CH)
+        nc.sync.dma_start(list_b[:], two)
+        nc.sync.dma_start(list_a[:], offs)
         for q in range(4):
             nc.sync.dma_start(
                 scale_win[32 * q : 32 * q + 4, :].bitcast(I32), x_scales[0, 4 * q : 4 * q + 4, :].bitcast(I32)
@@ -170,22 +171,25 @@ def tile_picked_crosscov_none_p_kernel(
         weave(nc.scalar.copy, w_a0[:], raw_a0[:])
         w_b1 = staged("w_b1", [P, HALF, PACK], BF16, woven_at)
         weave(nc.scalar.copy, w_b1[:], raw_b1[:])
-        w_a1 = sb("w_a1", [P, HALF, PACK], BF16)
-        weave(nc.scalar.copy, w_a1[:], raw_a1[:])
+        w_a2 = sb("w_a2", [P, CH, PACK], BF16)
+        weave(nc.scalar.copy, w_a2[:], raw_a1[:, :, 0:CH])
+        w_a3 = sb("w_a3", [P, CH, PACK], BF16)
+        weave(nc.scalar.copy, w_a3[:], raw_a1[:, :, CH:HALF])
 
-        xb_sc = sb("xb_sc", [P, S], U8)
-        xa_sc = sb("xa_sc", [P, S], U8)
-        pick_scales(xb_sc, list_b)
-        pick_scales(xa_sc, list_a)
+        picked_b, picked_a = sb("picked_b", [P, S], U8), sb("picked_a", [P, S], U8)
+        nc.vector.tensor_copy(picked_b[:], scale_win[:].indirect(list_b[:]))
+        nc.vector.tensor_copy(picked_a[:], scale_win[:].indirect(list_a[:]))
         q0_cd, q0_sc = sb("q0_cd", [P, CH], U32), sb("q0_sc", [P, CH], U8)
         quantise(q0_cd[:], q0_sc[:], w_q0[:])
+        xb_sc, xa_sc = sb("xb_sc", [P, S], U8), staged("xa_sc", [P, S], U8, q1_at + QUART // 2)
+        deal_scales(xb_sc, picked_b)
         xb_cd = sb("xb_cd", [P, S], U32)
         xa_cd = sb("xa_cd", [P, S], U32)
         pick_words(xb_cd, list_b)
         pick_words(xa_cd, list_a)
         z2_0 = staged("z2_0", [P, CH, PACK], BF16, q1_at)
         z2_1 = staged("z2_1", [P, CH, PACK], BF16, a0_at)
-        z_lo = staged("z_lo", [P, HALF, PACK], BF16, b1_at)
+        z_0 = staged("z_0", [P, CH, PACK], BF16, b1_at)
         z2_hi = staged("z2_hi", [P, HALF, PACK], BF16, a1_at)
         z2_cd, z2_sc = sb("z2_cd", [P, H], U32), staged("z2_sc", [P, H], U8, b1_at + RAW // 2)
 
@@ -193,6 +197,7 @@ def tile_picked_crosscov_none_p_kernel(
         q1_cd, q1_sc = sb("q1_cd", [P, CH], U32), sb("q1_sc", [P, CH], U8)
         quantise(q1_cd[:], q1_sc[:], w_q1[:])
         b1 = project_chunk(1, xb_cd, xb_sc, q1_cd[:], q1_sc[:])
+        deal_scales(xa_sc, picked_a)
         weigh_vector(z2_0[:], b0, gate_b)
         a0_cd, a0_sc = sb("a0_cd", [P, HALF], U32), sb("a0_sc", [P, HALF], U8)
         quantise(a0_cd[:], a0_sc[:], w_a0[:])
@@ -203,13 +208,15 @@ def tile_picked_crosscov_none_p_kernel(
         quantise(b1_cd[:], b1_sc[:], w_b1[:])
         b2 = project_chunk(2, xb_cd, xb_sc, b1_cd[:, 0:CH], b1_sc[:, 0:CH])
         b3 = project_chunk(3, xb_cd, xb_sc, b1_cd[:, CH:HALF], b1_sc[:, CH:HALF])
-        weigh_vector(z_lo[:, 0:CH, :], a0, gate_a)
+        weigh_vector(z_0[:], a0, gate_a)
+        a2_cd, a2_sc = sb("a2_cd", [P, CH], U32), sb("a2_sc", [P, CH], U8)
+        quantise(a2_cd[:], a2_sc[:], w_a2[:])
+        a2 = project_chunk(6, xa_cd, xa_sc, a2_cd[:], a2_sc[:])
         quantise(z2_cd[:, 0:CH], z2_sc[:, 0:CH], z2_0[:])
         quantise(z2_cd[:, CH:HALF], z2_sc[:, CH:HALF], z2_1[:])
-        a1_cd, a1_sc = sb("a1_cd", [P, HALF], U32), sb("a1_sc", [P, HALF], U8)
-        quantise(a1_cd[:], a1_sc[:], w_a1[:])
-        a2 = project_chunk(6, xa_cd, xa_sc, a1_cd[:, 0:CH], a1_sc[:, 0:CH])
-        a3 = project_chunk(7, xa_cd, xa_sc, a1_cd[:, CH:HALF], a1_sc[:, CH:HALF])
+        a3_cd, a3_sc = sb("a3_cd", [P, CH], U32), sb("a3_sc", [P, CH], U8)
+        quantise(a3_cd[:], a3_sc[:], w_a3[:])
+        a3 = project_chunk(7, xa_cd, xa_sc, a3_cd[:], a3_sc[:])
 
         pairs_a1 = staged("pairs_a1", [P, 2, CH, 2], BF16, woven_at)
         weigh_scalar_chunk(pairs_a1, a1, gate_a)
@@ -222,19 +229,24 @@ def tile_picked_crosscov_none_p_kernel(
 
         weigh_vector(z2_hi[:, 0:CH, :], b2, gate_b)
         weigh_vector(z2_hi[:, CH:HALF, :], b3, gate_b)
-        join_pairs(nc.vector.tensor_copy, F32, z_lo[:, CH:HALF, :], pairs_a1)
-        quantise(z2_cd[:, HALF:H], z2_sc[:, HALF:H], z2_hi[:])
         cv = {}
 
         def moments(c, i, codes, scales):
             cv[c] = bank(i, [P, H])
             product(cv[c][:], codes, scales, z2_cd[:], z2_sc[:])
 
-        zlo_cd = keep.tile([P, HALF], U32, name="zlo_cd", tag="z_cd", align_bytes=64)
-        zlo_sc = sb("zlo_sc", [P, HALF], U8)
-        quantise(zlo_cd[:], zlo_sc[:], z_lo[:])
-        moments(0, 0, zlo_cd[:, 0:CH], zlo_sc[:, 0:CH])
-        moments(1, 1, zlo_cd[:, CH:HALF], zlo_sc[:, CH:HALF])
+        z0_cd, z0_sc = sb("z0_cd", [P, CH], U32), staged("z0_sc", [P, CH], U8, a1_at + RAW // 2)
+        quantise(z0_cd[:], z0_sc[:], z_0[:])
+        cv[0] = bank(0, [P, H])
+        product(cv[0][:, 0:HALF], z0_cd[:], z0_sc[:], z2_cd[:, 0:HALF], z2_sc[:, 0:HALF])
+        z_1 = sb("z_1", [P, CH, PACK], BF16)
+        join_pairs(nc.vector.tensor_copy, F32, z_1[:], pairs_a1)
+        quantise(z2_cd[:, HALF:H], z2_sc[:, HALF:H], z2_hi[:])
+        product(cv[0][:, HALF:H], z0_cd[:], z0_sc[:], z2_cd[:, HALF:H], z2_sc[:, HALF:H])
+        z1_cd = keep.tile([P, CH], U32, name="z1_cd", tag="z_cd", align_bytes=64)
+        z1_sc = sb("z1_sc", [P, CH], U8)
+        quantise(z1_cd[:], z1_sc[:], z_1[:])
+        moments(1, 1, z1_cd[:], z1_sc[:])
         z_2 = sb("z_2", [P, CH, PACK], BF16)
         join_pairs(nc.vector.tensor_copy, F32, z_2[:], pairs_a2)
         z2c_cd, z2c_sc = sb("z2c_cd", [P, CH], U32), sb("z2c_sc", [P, CH], U8)

@@ -23,6 +23,7 @@ HALF = H // 2
 CH = 128
 LINE = 4
 RAW = 4 * PACK * HALF
+PLANE = 4
 
 
 def tile_picked_crosscov_none_p_kernel(
@@ -73,7 +74,7 @@ def tile_picked_crosscov_none_p_kernel(
             dst = bank(i, [P, PACK, CH])
             for t in range(PACK):
                 rows = slice(t * P, (t + 1) * P)
-                product(dst[:, t, :], x_cd[:, rows], x_sc[:, rows], w_cd, w_sc)
+                product(dst[:, t, :], x_cd[:, rows], x_sc[PLANE:P, rows], w_cd, w_sc)
             return dst
 
         def weigh_vector(dst, src, gate):
@@ -134,9 +135,9 @@ def tile_picked_crosscov_none_p_kernel(
         load_cols(raw_q0[:], wb, 0, CH)
         nc.sync.dma_start(list_b[:], two)
         nc.sync.dma_start(list_a[:], offs)
-        for q in range(4):
+        for q in (2, 3, 0, 1):
             nc.sync.dma_start(
-                scale_win[32 * q : 32 * q + 4, :].bitcast(I32), x_scales[0, 4 * q : 4 * q + 4, :].bitcast(I32)
+                scale_win[32 * q + PLANE : 32 * q + PLANE + 4, :].bitcast(I32), x_scales[0, 4 * q : 4 * q + 4, :].bitcast(I32)
             )
         word_win = staged("word_win", [P, T], U32, word_at)
         nc.sync.dma_start(word_win[:].bitcast(I32), x_words[0].rearrange("p n t -> p (n t)").bitcast(I32))
@@ -243,12 +244,12 @@ def tile_picked_crosscov_none_p_kernel(
         join_pairs(nc.vector.tensor_copy, F32, z_1[:], pairs_a1)
         quantise(z2_cd[:, HALF:H], z2_sc[:, HALF:H], z2_hi[:])
         product(cv[0][:, HALF:H], z0_cd[:], z0_sc[:], z2_cd[:, HALF:H], z2_sc[:, HALF:H])
+        z_2 = sb("z_2", [P, CH, PACK], BF16)
+        join_pairs(nc.vector.tensor_copy, F32, z_2[:], pairs_a2)
         z1_cd = keep.tile([P, CH], U32, name="z1_cd", tag="z_cd", align_bytes=64)
         z1_sc = sb("z1_sc", [P, CH], U8)
         quantise(z1_cd[:], z1_sc[:], z_1[:])
         moments(1, 1, z1_cd[:], z1_sc[:])
-        z_2 = sb("z_2", [P, CH, PACK], BF16)
-        join_pairs(nc.vector.tensor_copy, F32, z_2[:], pairs_a2)
         z2c_cd, z2c_sc = sb("z2c_cd", [P, CH], U32), sb("z2c_sc", [P, CH], U8)
         quantise(z2c_cd[:], z2c_sc[:], z_2[:])
         moments(2, 2, z2c_cd[:], z2c_sc[:])

@@ -18,7 +18,6 @@ COPY = mybir.ActivationFunctionType.Copy
 
 P = 128
 PACK = 4
-RUN = 8
 HALF = H // 2
 CH = 128
 LINE = 4
@@ -44,8 +43,15 @@ def tile_picked_crosscov_none_p_kernel(
         def bank(i, shape):
             return psum.tile(shape, F32, name="bank", tag="bank%d" % i)
 
-        def load_cols(dst, w, first, width):
-            nc.sync.dma_start(dst, w.rearrange("(p j) c -> p j c", j=PACK)[:, :, first : first + width])
+        def load_cols(name, w, first, width, offset):
+            raw = staged(name, [P, PACK, width], F32, offset)
+            nc.sync.dma_start(raw[:], w.rearrange("(p j) c -> p j c", j=PACK)[:, :, first : first + width])
+            return raw
+
+        def load_gate(name, g):
+            gate = sb(name, [P, PACK], F32)
+            nc.sync.dma_start(gate[:], g.rearrange("(p t) o -> p (t o)", t=PACK))
+            return gate
 
         def weave(copy, dst, src):
             copy(dst.rearrange("p (c i) j -> p c j i", i=LINE), src.rearrange("p j (c i) -> p c j i", i=LINE))
@@ -59,18 +65,10 @@ def tile_picked_crosscov_none_p_kernel(
                 start=True, stop=True,
             )
 
-        def pick_words(dst, places):
-            nc.vector.tensor_copy(
-                dst[:].rearrange("p (t b r) -> p b t r", t=PACK, r=RUN), word_win[:].indirect(places[:])
-            )
+        def pick(dst, window, places):
+            nc.vector.tensor_copy(dst[:].rearrange("p (t m) -> p m t", t=PACK), window[:].indirect(places[:]))
 
-        def deal_scales(dst, src):
-            nc.vector.tensor_copy(
-                dst[:].bitcast(I32).rearrange("p (t b r) -> p t b r", t=PACK, r=RUN // 4),
-                src[:].bitcast(I32).rearrange("p (b t r) -> p t b r", t=PACK, r=RUN // 4),
-            )
-
-        def project_chunk(i, x_cd, x_sc, w_cd, w_sc):
+        def project(i, x_cd, x_sc, w_cd, w_sc):
             dst = bank(i, [P, PACK, CH])
             for t in range(PACK):
                 rows = slice(t * P, (t + 1) * P)
@@ -81,11 +79,11 @@ def tile_picked_crosscov_none_p_kernel(
             nc.vector.tensor_tensor(
                 dst,
                 src[:].rearrange("p t n -> p n t"),
-                gate.rearrange("p (o t) -> p o t", o=1).to_broadcast([P, CH, PACK]),
+                gate[:].rearrange("p (o t) -> p o t", o=1).to_broadcast([P, CH, PACK]),
                 MULT,
             )
 
-        def weigh_scalar_chunk(pairs, src, gate):
+        def weigh_scalar(pairs, src, gate):
             for t in range(PACK):
                 nc.scalar.activation(pairs[:, t // 2, :, t % 2], src[:, t, :], COPY, scale=gate[:, t : t + 1])
 
@@ -103,161 +101,118 @@ def tile_picked_crosscov_none_p_kernel(
                 nc.vector.scalar_tensor_tensor(res[:], old_sb[c][:, cols], 0.75, cv[:, cols], MULT, ADD)
                 nc.sync.dma_start(out[c * P : (c + 1) * P, cols], res[:])
 
-        QUART = RAW // 2
-        q0_at, word_at = 0, QUART
-        q1_at = word_at + 2 * RAW
-        a0_at = q1_at + QUART
-        b1_at, a1_at, old_at, gate_at = a0_at + RAW, a0_at + 2 * RAW, a0_at + 3 * RAW, a0_at + 5 * RAW
+        def quantised(name, values, width):
+            codes, scales = sb(name + "_cd", [P, width], U32), sb(name + "_sc", [P, width], U8)
+            quantise(codes[:], scales[:], values)
+            return codes, scales
 
-        woven_at = gate_at + 4 * P
+        b0_at, b1_at, a01_at, b23_at, a23_at = 0, RAW // 2, RAW, 2 * RAW, 3 * RAW
+        lo, hi = slice(0, CH), slice(CH, HALF)
 
         list_b = keep.tile([P, S // 16], U16, name="list_b")
         list_a = keep.tile([P, S // 16], U16, name="list_a")
         scale_win = sb("scale_win", [P, T], U8)
-        ident = sb("ident", [P, P], F32)
-        zeros = staged("zeros", [P, (gate_at - word_at) // 4 + P], F32, word_at)
+        word_win = sb("word_win", [P, T], U32)
 
         nc.vector.memset(scale_win[:].bitcast(I32), 0)
-        nc.gpsimd.memset(zeros[:, 0:P], 0.0)
-        nc.gpsimd.affine_select(
-            out=ident[:],
-            in_=zeros[:, 0:P],
-            compare_op=mybir.AluOpType.not_equal,
-            fill=1.0,
-            base=0,
-            pattern=[[-1, P]],
-            channel_multiplier=1,
-        )
-        gate_rows = staged("gate_rows", [P, P], F32, gate_at)
-        nc.gpsimd.memset(gate_rows[:], 0.0)
-
-        raw_q0 = staged("raw_q0", [P, PACK, CH], F32, q0_at)
-        load_cols(raw_q0[:], wb, 0, CH)
+        raw_b0 = load_cols("raw_b0", wb, 0, CH, b0_at)
         nc.sync.dma_start(list_b[:], two)
         nc.sync.dma_start(list_a[:], offs)
-        for q in (2, 3, 0, 1):
-            nc.sync.dma_start(
-                scale_win[32 * q + PLANE : 32 * q + PLANE + 4, :].bitcast(I32), x_scales[0, 4 * q : 4 * q + 4, :].bitcast(I32)
-            )
-        word_win = staged("word_win", [P, T], U32, word_at)
+        for j in range(4):
+            nc.sync.dma_start(scale_win[PLANE + j : P : 32, :].bitcast(I32), x_scales[0, j:16:4, :].bitcast(I32))
         nc.sync.dma_start(word_win[:].bitcast(I32), x_words[0].rearrange("p n t -> p (n t)").bitcast(I32))
-        for i, g in enumerate((gt, gi)):
-            nc.sync.dma_start(
-                gate_rows[PACK * i : PACK * (i + 1), :].rearrange("t (b r) -> t b r", r=RUN),
-                g.rearrange("(b t r) o -> t b (r o)", t=PACK, r=RUN),
-            )
-        raw_q1 = staged("raw_q1", [P, PACK, CH], F32, q1_at)
-        load_cols(raw_q1[:], wb, CH, CH)
-        raw_a0 = staged("raw_a0", [P, PACK, HALF], F32, a0_at)
-        load_cols(raw_a0[:], wa, 0, HALF)
-        raw_b1 = staged("raw_b1", [P, PACK, HALF], F32, b1_at)
-        load_cols(raw_b1[:], wb, HALF, HALF)
-        raw_a1 = staged("raw_a1", [P, PACK, HALF], F32, a1_at)
-        load_cols(raw_a1[:], wa, HALF, HALF)
-        old_sb = [staged("old%d" % c, [P, H], F32, old_at + 4 * c * H) for c in range(4)]
+        raw_gate_b = load_gate("raw_gate_b", gi)
+        gate_a = load_gate("gate_a", gt)
+        raw_b1 = load_cols("raw_b1", wb, CH, CH, b1_at)
+        raw_a01 = load_cols("raw_a01", wa, 0, HALF, a01_at)
+        raw_b23 = load_cols("raw_b23", wb, HALF, HALF, b23_at)
+        raw_a23 = load_cols("raw_a23", wa, HALF, HALF, a23_at)
+        old_sb = [sb("old%d" % c, [P, H], F32) for c in range(4)]
         for c in range(4):
             nc.sync.dma_start(old_sb[c][:], old[c * P : (c + 1) * P, :])
 
-        gate_ps = bank(0, [P, P])
-        nc.tensor.transpose(gate_ps[:], gate_rows[:], ident[:])
-
-        w_q0 = sb("w_q0", [P, CH, PACK], BF16)
-        weave(nc.scalar.copy, w_q0[:], raw_q0[:])
-        gates = sb("gates", [P, 2 * PACK], F32)
-        nc.scalar.activation(gates[:], gate_ps[:, 0 : 2 * PACK], COPY, scale=0.125)
-        gate_a, gate_b = gates[:, 0:PACK], gates[:, PACK : 2 * PACK]
-        w_q1 = sb("w_q1", [P, CH, PACK], BF16)
-        weave(nc.scalar.copy, w_q1[:], raw_q1[:])
-        w_a0 = sb("w_a0", [P, HALF, PACK], BF16)
-        weave(nc.scalar.copy, w_a0[:], raw_a0[:])
-        w_b1 = staged("w_b1", [P, HALF, PACK], BF16, woven_at)
+        w_b0, w_b1 = sb("w_b0", [P, CH, PACK], BF16), sb("w_b1", [P, CH, PACK], BF16)
+        weave(nc.scalar.copy, w_b0[:], raw_b0[:])
+        gate_b = sb("gate_b", [P, PACK], F32)
+        nc.scalar.activation(gate_b[:], raw_gate_b[:], COPY, scale=1.0 / 64)
         weave(nc.scalar.copy, w_b1[:], raw_b1[:])
-        w_a2 = sb("w_a2", [P, CH, PACK], BF16)
-        weave(nc.scalar.copy, w_a2[:], raw_a1[:, :, 0:CH])
-        w_a3 = sb("w_a3", [P, CH, PACK], BF16)
-        weave(nc.scalar.copy, w_a3[:], raw_a1[:, :, CH:HALF])
+        w_a01 = sb("w_a01", [P, HALF, PACK], BF16)
+        weave(nc.scalar.copy, w_a01[:], raw_a01[:])
+        w_b23 = staged("w_b23", [P, HALF, PACK], BF16, 4 * RAW)
+        weave(nc.scalar.copy, w_b23[:], raw_b23[:])
+        w_a2, w_a3 = sb("w_a2", [P, CH, PACK], BF16), sb("w_a3", [P, CH, PACK], BF16)
+        weave(nc.scalar.copy, w_a2[:], raw_a23[:, :, lo])
+        weave(nc.scalar.copy, w_a3[:], raw_a23[:, :, hi])
 
-        picked_b, picked_a = sb("picked_b", [P, S], U8), sb("picked_a", [P, S], U8)
-        nc.vector.tensor_copy(picked_b[:], scale_win[:].indirect(list_b[:]))
-        nc.vector.tensor_copy(picked_a[:], scale_win[:].indirect(list_a[:]))
-        q0_cd, q0_sc = sb("q0_cd", [P, CH], U32), sb("q0_sc", [P, CH], U8)
-        quantise(q0_cd[:], q0_sc[:], w_q0[:])
-        xb_sc, xa_sc = sb("xb_sc", [P, S], U8), staged("xa_sc", [P, S], U8, q1_at + QUART // 2)
-        deal_scales(xb_sc, picked_b)
-        xb_cd = sb("xb_cd", [P, S], U32)
-        xa_cd = sb("xa_cd", [P, S], U32)
-        pick_words(xb_cd, list_b)
-        pick_words(xa_cd, list_a)
-        z2_0 = staged("z2_0", [P, CH, PACK], BF16, q1_at)
-        z2_1 = staged("z2_1", [P, CH, PACK], BF16, a0_at)
-        z_0 = staged("z_0", [P, CH, PACK], BF16, b1_at)
-        z2_hi = staged("z2_hi", [P, HALF, PACK], BF16, a1_at)
-        z2_cd, z2_sc = sb("z2_cd", [P, H], U32), staged("z2_sc", [P, H], U8, b1_at + RAW // 2)
+        xb_sc, xa_sc = sb("xb_sc", [P, S], U8), sb("xa_sc", [P, S], U8)
+        xb_cd, xa_cd = sb("xb_cd", [P, S], U32), sb("xa_cd", [P, S], U32)
+        pick(xb_sc, scale_win, list_b)
+        pick(xa_sc, scale_win, list_a)
+        b0_cd, b0_sc = quantised("b0", w_b0[:], CH)
+        pick(xb_cd, word_win, list_b)
+        pick(xa_cd, word_win, list_a)
 
-        b0 = project_chunk(0, xb_cd, xb_sc, q0_cd[:], q0_sc[:])
-        q1_cd, q1_sc = sb("q1_cd", [P, CH], U32), sb("q1_sc", [P, CH], U8)
-        quantise(q1_cd[:], q1_sc[:], w_q1[:])
-        b1 = project_chunk(1, xb_cd, xb_sc, q1_cd[:], q1_sc[:])
-        deal_scales(xa_sc, picked_a)
+        z2_0 = staged("z2_0", [P, CH, PACK], BF16, b1_at)
+        z2_1 = staged("z2_1", [P, CH, PACK], BF16, a01_at)
+        z_0 = staged("z_0", [P, CH, PACK], BF16, b23_at)
+        z2_hi = staged("z2_hi", [P, HALF, PACK], BF16, a23_at)
+        z2_cd, z2_sc = sb("z2_cd", [P, H], U32), staged("z2_sc", [P, H], U8, b23_at + RAW // 2)
+
+        b0 = project(0, xb_cd, xb_sc, b0_cd[:], b0_sc[:])
+        cd, sc = quantised("b1", w_b1[:], CH)
+        b1 = project(1, xb_cd, xb_sc, cd[:], sc[:])
         weigh_vector(z2_0[:], b0, gate_b)
-        a0_cd, a0_sc = sb("a0_cd", [P, HALF], U32), sb("a0_sc", [P, HALF], U8)
-        quantise(a0_cd[:], a0_sc[:], w_a0[:])
-        a0 = project_chunk(4, xa_cd, xa_sc, a0_cd[:, 0:CH], a0_sc[:, 0:CH])
-        a1 = project_chunk(5, xa_cd, xa_sc, a0_cd[:, CH:HALF], a0_sc[:, CH:HALF])
+        cd, sc = quantised("a01", w_a01[:], HALF)
+        a0 = project(4, xa_cd, xa_sc, cd[:, lo], sc[:, lo])
+        a1 = project(5, xa_cd, xa_sc, cd[:, hi], sc[:, hi])
         weigh_vector(z2_1[:], b1, gate_b)
-        b1_cd, b1_sc = sb("b1_cd", [P, HALF], U32), sb("b1_sc", [P, HALF], U8)
-        quantise(b1_cd[:], b1_sc[:], w_b1[:])
-        b2 = project_chunk(2, xb_cd, xb_sc, b1_cd[:, 0:CH], b1_sc[:, 0:CH])
-        b3 = project_chunk(3, xb_cd, xb_sc, b1_cd[:, CH:HALF], b1_sc[:, CH:HALF])
+        cd, sc = quantised("b23", w_b23[:], HALF)
+        b2 = project(2, xb_cd, xb_sc, cd[:, lo], sc[:, lo])
+        b3 = project(3, xb_cd, xb_sc, cd[:, hi], sc[:, hi])
         weigh_vector(z_0[:], a0, gate_a)
-        a2_cd, a2_sc = sb("a2_cd", [P, CH], U32), sb("a2_sc", [P, CH], U8)
-        quantise(a2_cd[:], a2_sc[:], w_a2[:])
-        a2 = project_chunk(6, xa_cd, xa_sc, a2_cd[:], a2_sc[:])
+        cd, sc = quantised("a2", w_a2[:], CH)
+        a2 = project(6, xa_cd, xa_sc, cd[:], sc[:])
         quantise(z2_cd[:, 0:CH], z2_sc[:, 0:CH], z2_0[:])
         quantise(z2_cd[:, CH:HALF], z2_sc[:, CH:HALF], z2_1[:])
-        a3_cd, a3_sc = sb("a3_cd", [P, CH], U32), sb("a3_sc", [P, CH], U8)
-        quantise(a3_cd[:], a3_sc[:], w_a3[:])
-        a3 = project_chunk(7, xa_cd, xa_sc, a3_cd[:], a3_sc[:])
+        cd, sc = quantised("a3", w_a3[:], CH)
+        a3 = project(7, xa_cd, xa_sc, cd[:], sc[:])
 
-        pairs_a1 = staged("pairs_a1", [P, 2, CH, 2], BF16, woven_at)
-        weigh_scalar_chunk(pairs_a1, a1, gate_a)
-        pairs_a2 = sb("pairs_a2", [P, 2, CH, 2], BF16)
-        weigh_scalar_chunk(pairs_a2, a2, gate_a)
-        pairs_a3 = sb("pairs_a3", [P, 2, CH, 2], BF16)
-        weigh_scalar_chunk(pairs_a3, a3, gate_a)
+        pairs_a1 = staged("pairs_a1", [P, 2, CH, 2], BF16, 4 * RAW)
+        weigh_scalar(pairs_a1, a1, gate_a)
+        pairs_a2, pairs_a3 = sb("pairs_a2", [P, 2, CH, 2], BF16), sb("pairs_a3", [P, 2, CH, 2], BF16)
+        weigh_scalar(pairs_a2, a2, gate_a)
+        weigh_scalar(pairs_a3, a3, gate_a)
         z_3 = sb("z_3", [P, CH, PACK], BF16)
         join_pairs(nc.scalar.copy, U32, z_3[:], pairs_a3)
 
-        weigh_vector(z2_hi[:, 0:CH, :], b2, gate_b)
-        weigh_vector(z2_hi[:, CH:HALF, :], b3, gate_b)
-        cv = {}
+        weigh_vector(z2_hi[:, lo, :], b2, gate_b)
+        weigh_vector(z2_hi[:, hi, :], b3, gate_b)
 
-        def moments(c, i, codes, scales):
-            cv[c] = bank(i, [P, H])
-            product(cv[c][:], codes, scales, z2_cd[:], z2_sc[:])
+        def moments(i, codes, scales):
+            cv = bank(i, [P, H])
+            product(cv[:], codes[:], scales[:], z2_cd[:], z2_sc[:])
+            return cv
 
-        z0_cd, z0_sc = sb("z0_cd", [P, CH], U32), staged("z0_sc", [P, CH], U8, a1_at + RAW // 2)
+        z0_cd, z0_sc = sb("z0_cd", [P, CH], U32), staged("z0_sc", [P, CH], U8, a23_at + RAW // 2)
         quantise(z0_cd[:], z0_sc[:], z_0[:])
-        cv[0] = bank(0, [P, H])
-        product(cv[0][:, 0:HALF], z0_cd[:], z0_sc[:], z2_cd[:, 0:HALF], z2_sc[:, 0:HALF])
+        cv0 = bank(0, [P, H])
+        product(cv0[:, 0:HALF], z0_cd[:], z0_sc[:], z2_cd[:, 0:HALF], z2_sc[:, 0:HALF])
         z_1 = sb("z_1", [P, CH, PACK], BF16)
         join_pairs(nc.vector.tensor_copy, F32, z_1[:], pairs_a1)
         quantise(z2_cd[:, HALF:H], z2_sc[:, HALF:H], z2_hi[:])
-        product(cv[0][:, HALF:H], z0_cd[:], z0_sc[:], z2_cd[:, HALF:H], z2_sc[:, HALF:H])
+        product(cv0[:, HALF:H], z0_cd[:], z0_sc[:], z2_cd[:, HALF:H], z2_sc[:, HALF:H])
         z_2 = sb("z_2", [P, CH, PACK], BF16)
         join_pairs(nc.vector.tensor_copy, F32, z_2[:], pairs_a2)
         z1_cd = keep.tile([P, CH], U32, name="z1_cd", tag="z_cd", align_bytes=64)
         z1_sc = sb("z1_sc", [P, CH], U8)
         quantise(z1_cd[:], z1_sc[:], z_1[:])
-        moments(1, 1, z1_cd[:], z1_sc[:])
-        z2c_cd, z2c_sc = sb("z2c_cd", [P, CH], U32), sb("z2c_sc", [P, CH], U8)
-        quantise(z2c_cd[:], z2c_sc[:], z_2[:])
-        moments(2, 2, z2c_cd[:], z2c_sc[:])
-        finish(0, cv[0], 1)
+        cv1 = moments(1, z1_cd, z1_sc)
+        cv2 = moments(2, *quantised("z2c", z_2[:], CH))
+        finish(0, cv0, 1)
         z3_cd = keep.tile([P, CH], U32, name="z3_cd", tag="z_cd", align_bytes=64)
         z3_sc = sb("z3_sc", [P, CH], U8)
         quantise(z3_cd[:], z3_sc[:], z_3[:])
-        moments(3, 3, z3_cd[:], z3_sc[:])
-        finish(1, cv[1], 1)
-        finish(2, cv[2], 1)
-        finish(3, cv[3], 2)
+        cv3 = moments(3, z3_cd, z3_sc)
+        finish(1, cv1, 1)
+        finish(2, cv2, 1)
+        finish(3, cv3, 2)

@@ -23,6 +23,7 @@ CH = 128
 LINE = 4
 RAW = 4 * PACK * HALF
 PLANE = 4
+SHARE = 0.25 * 0.0625
 
 
 def tile_picked_crosscov_none_p_kernel(
@@ -75,11 +76,13 @@ def tile_picked_crosscov_none_p_kernel(
                 product(dst[:, t, :], x_cd[:, rows], x_sc[PLANE:P, rows], w_cd, w_sc)
             return dst
 
-        def weigh_vector(dst, src, gate):
-            nc.vector.tensor_tensor(
+        def weigh_vector(dst, src, gate, factor):
+            nc.vector.scalar_tensor_tensor(
                 dst,
                 src[:].rearrange("p t n -> p n t"),
+                factor,
                 gate[:].rearrange("p (o t) -> p o t", o=1).to_broadcast([P, CH, PACK]),
+                MULT,
                 MULT,
             )
 
@@ -93,13 +96,11 @@ def tile_picked_crosscov_none_p_kernel(
                 pairs[:].rearrange("p u n e -> p u (n e)").bitcast(word).rearrange("p u n -> p n u"),
             )
 
-        def finish(c, cv, pieces):
-            width = H // pieces
-            for i in range(pieces):
-                cols = slice(i * width, (i + 1) * width)
-                res = sb("res%d_%d" % (c, i), [P, width], F32)
-                nc.vector.scalar_tensor_tensor(res[:], old_sb[c][:, cols], 0.75, cv[:, cols], MULT, ADD)
-                nc.sync.dma_start(out[c * P : (c + 1) * P, cols], res[:])
+        def finish(c, cv, first, width):
+            cols = slice(first, first + width)
+            res = sb("res%d_%d" % (c, first), [P, width], F32)
+            nc.vector.scalar_tensor_tensor(res[:], old_sb[c][:, cols], 0.75, cv, MULT, ADD)
+            nc.sync.dma_start(out[c * P : (c + 1) * P, cols], res[:])
 
         def quantised(name, values, width):
             codes, scales = sb(name + "_cd", [P, width], U32), sb(name + "_sc", [P, width], U8)
@@ -117,13 +118,13 @@ def tile_picked_crosscov_none_p_kernel(
         nc.vector.memset(scale_win[:].bitcast(I32), 0)
         raw_b0 = load_cols("raw_b0", wb, 0, CH, b0_at)
         nc.sync.dma_start(list_b[:], two)
-        nc.sync.dma_start(list_a[:], offs)
         for j in range(4):
             nc.sync.dma_start(scale_win[PLANE + j : P : 32, :].bitcast(I32), x_scales[0, j:16:4, :].bitcast(I32))
+        nc.sync.dma_start(list_a[:], offs)
         nc.sync.dma_start(word_win[:].bitcast(I32), x_words[0].rearrange("p n t -> p (n t)").bitcast(I32))
-        raw_gate_b = load_gate("raw_gate_b", gi)
-        gate_a = load_gate("gate_a", gt)
         raw_b1 = load_cols("raw_b1", wb, CH, CH, b1_at)
+        gate_b = load_gate("gate_b", gi)
+        gate_a = load_gate("gate_a", gt)
         raw_a01 = load_cols("raw_a01", wa, 0, HALF, a01_at)
         raw_b23 = load_cols("raw_b23", wb, HALF, HALF, b23_at)
         raw_a23 = load_cols("raw_a23", wa, HALF, HALF, a23_at)
@@ -133,8 +134,6 @@ def tile_picked_crosscov_none_p_kernel(
 
         w_b0, w_b1 = sb("w_b0", [P, CH, PACK], BF16), sb("w_b1", [P, CH, PACK], BF16)
         weave(nc.scalar.copy, w_b0[:], raw_b0[:])
-        gate_b = sb("gate_b", [P, PACK], F32)
-        nc.scalar.activation(gate_b[:], raw_gate_b[:], COPY, scale=1.0 / 64)
         weave(nc.scalar.copy, w_b1[:], raw_b1[:])
         w_a01 = sb("w_a01", [P, HALF, PACK], BF16)
         weave(nc.scalar.copy, w_a01[:], raw_a01[:])
@@ -161,15 +160,15 @@ def tile_picked_crosscov_none_p_kernel(
         b0 = project(0, xb_cd, xb_sc, b0_cd[:], b0_sc[:])
         cd, sc = quantised("b1", w_b1[:], CH)
         b1 = project(1, xb_cd, xb_sc, cd[:], sc[:])
-        weigh_vector(z2_0[:], b0, gate_b)
+        weigh_vector(z2_0[:], b0, gate_b, SHARE)
         cd, sc = quantised("a01", w_a01[:], HALF)
         a0 = project(4, xa_cd, xa_sc, cd[:, lo], sc[:, lo])
         a1 = project(5, xa_cd, xa_sc, cd[:, hi], sc[:, hi])
-        weigh_vector(z2_1[:], b1, gate_b)
+        weigh_vector(z2_1[:], b1, gate_b, SHARE)
         cd, sc = quantised("b23", w_b23[:], HALF)
         b2 = project(2, xb_cd, xb_sc, cd[:, lo], sc[:, lo])
         b3 = project(3, xb_cd, xb_sc, cd[:, hi], sc[:, hi])
-        weigh_vector(z_0[:], a0, gate_a)
+        weigh_vector(z_0[:], a0, gate_a, 1.0)
         cd, sc = quantised("a2", w_a2[:], CH)
         a2 = project(6, xa_cd, xa_sc, cd[:], sc[:])
         quantise(z2_cd[:, 0:CH], z2_sc[:, 0:CH], z2_0[:])
@@ -185,34 +184,37 @@ def tile_picked_crosscov_none_p_kernel(
         z_3 = sb("z_3", [P, CH, PACK], BF16)
         join_pairs(nc.scalar.copy, U32, z_3[:], pairs_a3)
 
-        weigh_vector(z2_hi[:, lo, :], b2, gate_b)
-        weigh_vector(z2_hi[:, hi, :], b3, gate_b)
+        weigh_vector(z2_hi[:, lo, :], b2, gate_b, SHARE)
+        weigh_vector(z2_hi[:, hi, :], b3, gate_b, SHARE)
 
-        def moments(i, codes, scales):
-            cv = bank(i, [P, H])
-            product(cv[:], codes[:], scales[:], z2_cd[:], z2_sc[:])
-            return cv
+        def moments(cv, codes, scales, first, width):
+            cols = slice(first, first + width)
+            product(cv, codes[:], scales[:], z2_cd[:, cols], z2_sc[:, cols])
 
-        z0_cd, z0_sc = sb("z0_cd", [P, CH], U32), staged("z0_sc", [P, CH], U8, a23_at + RAW // 2)
-        quantise(z0_cd[:], z0_sc[:], z_0[:])
-        cv0 = bank(0, [P, H])
-        product(cv0[:, 0:HALF], z0_cd[:], z0_sc[:], z2_cd[:, 0:HALF], z2_sc[:, 0:HALF])
         z_1 = sb("z_1", [P, CH, PACK], BF16)
         join_pairs(nc.vector.tensor_copy, F32, z_1[:], pairs_a1)
+        z0_cd = keep.tile([P, CH], U32, name="z0_cd", tag="z_cd", align_bytes=64)
+        z0_sc = staged("z0_sc", [P, CH], U8, a23_at + RAW // 2)
+        quantise(z0_cd[:], z0_sc[:], z_0[:])
+        cv0_lo, cv0_hi, cv1 = bank(0, [P, HALF]), bank(4, [P, HALF]), bank(1, [P, H])
+        moments(cv0_lo[:], z0_cd, z0_sc, 0, HALF)
+        z1_cd, z1_sc = quantised("z1", z_1[:], CH)
+        moments(cv1[:, 0:HALF], z1_cd, z1_sc, 0, HALF)
         quantise(z2_cd[:, HALF:H], z2_sc[:, HALF:H], z2_hi[:])
-        product(cv0[:, HALF:H], z0_cd[:], z0_sc[:], z2_cd[:, HALF:H], z2_sc[:, HALF:H])
+        moments(cv0_hi[:], z0_cd, z0_sc, HALF, HALF)
+        moments(cv1[:, HALF:H], z1_cd, z1_sc, HALF, HALF)
         z_2 = sb("z_2", [P, CH, PACK], BF16)
         join_pairs(nc.vector.tensor_copy, F32, z_2[:], pairs_a2)
-        z1_cd = keep.tile([P, CH], U32, name="z1_cd", tag="z_cd", align_bytes=64)
-        z1_sc = sb("z1_sc", [P, CH], U8)
-        quantise(z1_cd[:], z1_sc[:], z_1[:])
-        cv1 = moments(1, z1_cd, z1_sc)
-        cv2 = moments(2, *quantised("z2c", z_2[:], CH))
-        finish(0, cv0, 1)
+        finish(0, cv0_lo[:], 0, HALF)
+        cv2 = bank(2, [P, H])
+        moments(cv2[:], *quantised("z2c", z_2[:], CH), 0, H)
+        finish(0, cv0_hi[:], HALF, HALF)
         z3_cd = keep.tile([P, CH], U32, name="z3_cd", tag="z_cd", align_bytes=64)
         z3_sc = sb("z3_sc", [P, CH], U8)
         quantise(z3_cd[:], z3_sc[:], z_3[:])
-        cv3 = moments(3, z3_cd, z3_sc)
-        finish(1, cv1, 1)
-        finish(2, cv2, 1)
-        finish(3, cv3, 2)
+        cv3 = bank(3, [P, H])
+        moments(cv3[:], z3_cd, z3_sc, 0, H)
+        finish(1, cv1[:], 0, H)
+        finish(2, cv2[:], 0, H)
+        finish(3, cv3[:, 0:HALF], 0, HALF)
+        finish(3, cv3[:, HALF:H], HALF, HALF)

@@ -23,7 +23,6 @@ CH = 128
 LINE = 4
 RAW = 4 * PACK * HALF
 PLANE = 4
-SHARE = 0.25 * 0.0625
 
 
 def tile_picked_crosscov_none_p_kernel(
@@ -76,13 +75,11 @@ def tile_picked_crosscov_none_p_kernel(
                 product(dst[:, t, :], x_cd[:, rows], x_sc[PLANE:P, rows], w_cd, w_sc)
             return dst
 
-        def weigh_vector(dst, src, gate, factor):
-            nc.vector.scalar_tensor_tensor(
+        def weigh_vector(dst, src, gate):
+            nc.vector.tensor_tensor(
                 dst,
                 src[:].rearrange("p t n -> p n t"),
-                factor,
                 gate[:].rearrange("p (o t) -> p o t", o=1).to_broadcast([P, CH, PACK]),
-                MULT,
                 MULT,
             )
 
@@ -96,11 +93,13 @@ def tile_picked_crosscov_none_p_kernel(
                 pairs[:].rearrange("p u n e -> p u (n e)").bitcast(word).rearrange("p u n -> p n u"),
             )
 
-        def finish(c, cv, first, width):
-            cols = slice(first, first + width)
-            res = sb("res%d_%d" % (c, first), [P, width], F32)
-            nc.vector.scalar_tensor_tensor(res[:], old_sb[c][:, cols], 0.75, cv, MULT, ADD)
-            nc.sync.dma_start(out[c * P : (c + 1) * P, cols], res[:])
+        def finish(c, cv, pieces):
+            width = H // pieces
+            for i in range(pieces):
+                cols = slice(i * width, (i + 1) * width)
+                res = sb("res%d_%d" % (c, i), [P, width], F32)
+                nc.vector.scalar_tensor_tensor(res[:], old_sb[c][:, cols], 0.75, cv[:, cols], MULT, ADD)
+                nc.sync.dma_start(out[c * P : (c + 1) * P, cols], res[:])
 
         def quantised(name, values, width):
             codes, scales = sb(name + "_cd", [P, width], U32), sb(name + "_sc", [P, width], U8)
@@ -116,30 +115,31 @@ def tile_picked_crosscov_none_p_kernel(
         word_win = sb("word_win", [P, T], U32)
 
         nc.vector.memset(scale_win[:].bitcast(I32), 0)
-        raw_b0 = load_cols("raw_b0", wb, 0, CH, b0_at)
         nc.sync.dma_start(list_b[:], two)
+        raw_b0 = load_cols("raw_b0", wb, 0, CH, b0_at)
+        nc.sync.dma_start(list_a[:], offs)
         for j in range(4):
             nc.sync.dma_start(scale_win[PLANE + j : P : 32, :].bitcast(I32), x_scales[0, j:16:4, :].bitcast(I32))
-        nc.sync.dma_start(list_a[:], offs)
-        nc.sync.dma_start(word_win[:].bitcast(I32), x_words[0].rearrange("p n t -> p (n t)").bitcast(I32))
         raw_b1 = load_cols("raw_b1", wb, CH, CH, b1_at)
-        gate_b = load_gate("gate_b", gi)
-        gate_a = load_gate("gate_a", gt)
+        nc.sync.dma_start(word_win[:].bitcast(I32), x_words[0].rearrange("p n t -> p (n t)").bitcast(I32))
         raw_a01 = load_cols("raw_a01", wa, 0, HALF, a01_at)
+        raw_gate_b = load_gate("raw_gate_b", gi)
+        gate_a = load_gate("gate_a", gt)
         raw_b23 = load_cols("raw_b23", wb, HALF, HALF, b23_at)
         raw_a23 = load_cols("raw_a23", wa, HALF, HALF, a23_at)
         old_sb = [sb("old%d" % c, [P, H], F32) for c in range(4)]
         for c in range(4):
             nc.sync.dma_start(old_sb[c][:], old[c * P : (c + 1) * P, :])
 
-        w_b0, w_b1 = sb("w_b0", [P, CH, PACK], BF16), sb("w_b1", [P, CH, PACK], BF16)
-        weave(nc.scalar.copy, w_b0[:], raw_b0[:])
-        weave(nc.scalar.copy, w_b1[:], raw_b1[:])
-        w_a01 = sb("w_a01", [P, HALF, PACK], BF16)
-        weave(nc.scalar.copy, w_a01[:], raw_a01[:])
+        w_b01, w_a01 = sb("w_b01", [P, HALF, PACK], BF16), sb("w_a01", [P, HALF, PACK], BF16)
         w_b23 = staged("w_b23", [P, HALF, PACK], BF16, 4 * RAW)
-        weave(nc.scalar.copy, w_b23[:], raw_b23[:])
         w_a2, w_a3 = sb("w_a2", [P, CH, PACK], BF16), sb("w_a3", [P, CH, PACK], BF16)
+        weave(nc.scalar.copy, w_b01[:, lo, :], raw_b0[:])
+        weave(nc.scalar.copy, w_b01[:, hi, :], raw_b1[:])
+        weave(nc.scalar.copy, w_a01[:], raw_a01[:])
+        gate_b = sb("gate_b", [P, PACK], F32)
+        nc.scalar.activation(gate_b[:], raw_gate_b[:], COPY, scale=1.0 / 64)
+        weave(nc.scalar.copy, w_b23[:], raw_b23[:])
         weave(nc.scalar.copy, w_a2[:], raw_a23[:, :, lo])
         weave(nc.scalar.copy, w_a3[:], raw_a23[:, :, hi])
 
@@ -147,34 +147,31 @@ def tile_picked_crosscov_none_p_kernel(
         xb_cd, xa_cd = sb("xb_cd", [P, S], U32), sb("xa_cd", [P, S], U32)
         pick(xb_sc, scale_win, list_b)
         pick(xa_sc, scale_win, list_a)
-        b0_cd, b0_sc = quantised("b0", w_b0[:], CH)
+        b01_cd, b01_sc = quantised("b01", w_b01[:], HALF)
         pick(xb_cd, word_win, list_b)
         pick(xa_cd, word_win, list_a)
 
-        z2_0 = staged("z2_0", [P, CH, PACK], BF16, b1_at)
-        z2_1 = staged("z2_1", [P, CH, PACK], BF16, a01_at)
+        z2_lo = staged("z2_lo", [P, HALF, PACK], BF16, a01_at)
         z_0 = staged("z_0", [P, CH, PACK], BF16, b23_at)
         z2_hi = staged("z2_hi", [P, HALF, PACK], BF16, a23_at)
         z2_cd, z2_sc = sb("z2_cd", [P, H], U32), staged("z2_sc", [P, H], U8, b23_at + RAW // 2)
 
-        b0 = project(0, xb_cd, xb_sc, b0_cd[:], b0_sc[:])
-        cd, sc = quantised("b1", w_b1[:], CH)
-        b1 = project(1, xb_cd, xb_sc, cd[:], sc[:])
-        weigh_vector(z2_0[:], b0, gate_b, SHARE)
+        b0 = project(0, xb_cd, xb_sc, b01_cd[:, lo], b01_sc[:, lo])
+        b1 = project(1, xb_cd, xb_sc, b01_cd[:, hi], b01_sc[:, hi])
         cd, sc = quantised("a01", w_a01[:], HALF)
-        a0 = project(4, xa_cd, xa_sc, cd[:, lo], sc[:, lo])
         a1 = project(5, xa_cd, xa_sc, cd[:, hi], sc[:, hi])
-        weigh_vector(z2_1[:], b1, gate_b, SHARE)
+        a0 = project(4, xa_cd, xa_sc, cd[:, lo], sc[:, lo])
+        weigh_vector(z2_lo[:, lo, :], b0, gate_b)
+        weigh_vector(z2_lo[:, hi, :], b1, gate_b)
         cd, sc = quantised("b23", w_b23[:], HALF)
         b2 = project(2, xb_cd, xb_sc, cd[:, lo], sc[:, lo])
         b3 = project(3, xb_cd, xb_sc, cd[:, hi], sc[:, hi])
-        weigh_vector(z_0[:], a0, gate_a, 1.0)
         cd, sc = quantised("a2", w_a2[:], CH)
         a2 = project(6, xa_cd, xa_sc, cd[:], sc[:])
-        quantise(z2_cd[:, 0:CH], z2_sc[:, 0:CH], z2_0[:])
-        quantise(z2_cd[:, CH:HALF], z2_sc[:, CH:HALF], z2_1[:])
+        weigh_vector(z_0[:], a0, gate_a)
         cd, sc = quantised("a3", w_a3[:], CH)
         a3 = project(7, xa_cd, xa_sc, cd[:], sc[:])
+        quantise(z2_cd[:, 0:HALF], z2_sc[:, 0:HALF], z2_lo[:])
 
         pairs_a1 = staged("pairs_a1", [P, 2, CH, 2], BF16, 4 * RAW)
         weigh_scalar(pairs_a1, a1, gate_a)
@@ -184,37 +181,34 @@ def tile_picked_crosscov_none_p_kernel(
         z_3 = sb("z_3", [P, CH, PACK], BF16)
         join_pairs(nc.scalar.copy, U32, z_3[:], pairs_a3)
 
-        weigh_vector(z2_hi[:, lo, :], b2, gate_b, SHARE)
-        weigh_vector(z2_hi[:, hi, :], b3, gate_b, SHARE)
+        weigh_vector(z2_hi[:, lo, :], b2, gate_b)
+        weigh_vector(z2_hi[:, hi, :], b3, gate_b)
 
-        def moments(cv, codes, scales, first, width):
-            cols = slice(first, first + width)
-            product(cv, codes[:], scales[:], z2_cd[:, cols], z2_sc[:, cols])
+        def moments(i, codes, scales):
+            cv = bank(i, [P, H])
+            product(cv[:], codes[:], scales[:], z2_cd[:], z2_sc[:])
+            return cv
 
+        z0_cd, z0_sc = sb("z0_cd", [P, CH], U32), staged("z0_sc", [P, CH], U8, a23_at + RAW // 2)
+        quantise(z0_cd[:], z0_sc[:], z_0[:])
+        cv0 = bank(0, [P, H])
+        product(cv0[:, 0:HALF], z0_cd[:], z0_sc[:], z2_cd[:, 0:HALF], z2_sc[:, 0:HALF])
         z_1 = sb("z_1", [P, CH, PACK], BF16)
         join_pairs(nc.vector.tensor_copy, F32, z_1[:], pairs_a1)
-        z0_cd = keep.tile([P, CH], U32, name="z0_cd", tag="z_cd", align_bytes=64)
-        z0_sc = staged("z0_sc", [P, CH], U8, a23_at + RAW // 2)
-        quantise(z0_cd[:], z0_sc[:], z_0[:])
-        cv0_lo, cv0_hi, cv1 = bank(0, [P, HALF]), bank(4, [P, HALF]), bank(1, [P, H])
-        moments(cv0_lo[:], z0_cd, z0_sc, 0, HALF)
-        z1_cd, z1_sc = quantised("z1", z_1[:], CH)
-        moments(cv1[:, 0:HALF], z1_cd, z1_sc, 0, HALF)
         quantise(z2_cd[:, HALF:H], z2_sc[:, HALF:H], z2_hi[:])
-        moments(cv0_hi[:], z0_cd, z0_sc, HALF, HALF)
-        moments(cv1[:, HALF:H], z1_cd, z1_sc, HALF, HALF)
+        product(cv0[:, HALF:H], z0_cd[:], z0_sc[:], z2_cd[:, HALF:H], z2_sc[:, HALF:H])
         z_2 = sb("z_2", [P, CH, PACK], BF16)
         join_pairs(nc.vector.tensor_copy, F32, z_2[:], pairs_a2)
-        finish(0, cv0_lo[:], 0, HALF)
-        cv2 = bank(2, [P, H])
-        moments(cv2[:], *quantised("z2c", z_2[:], CH), 0, H)
-        finish(0, cv0_hi[:], HALF, HALF)
+        z1_cd = keep.tile([P, CH], U32, name="z1_cd", tag="z_cd", align_bytes=64)
+        z1_sc = sb("z1_sc", [P, CH], U8)
+        quantise(z1_cd[:], z1_sc[:], z_1[:])
+        cv1 = moments(1, z1_cd, z1_sc)
+        cv2 = moments(2, *quantised("z2c", z_2[:], CH))
+        finish(0, cv0, 1)
         z3_cd = keep.tile([P, CH], U32, name="z3_cd", tag="z_cd", align_bytes=64)
         z3_sc = sb("z3_sc", [P, CH], U8)
         quantise(z3_cd[:], z3_sc[:], z_3[:])
-        cv3 = bank(3, [P, H])
-        moments(cv3[:], z3_cd, z3_sc, 0, H)
-        finish(1, cv1[:], 0, H)
-        finish(2, cv2[:], 0, H)
-        finish(3, cv3[:, 0:HALF], 0, HALF)
-        finish(3, cv3[:, HALF:H], HALF, HALF)
+        cv3 = moments(3, z3_cd, z3_sc)
+        finish(1, cv1, 1)
+        finish(2, cv2, 1)
+        finish(3, cv3, 2)

@@ -93,13 +93,11 @@ def tile_picked_crosscov_none_p_kernel(
                 pairs[:].rearrange("p u n e -> p u (n e)").bitcast(word).rearrange("p u n -> p n u"),
             )
 
-        def finish(c, cv, pieces):
-            width = H // pieces
-            for i in range(pieces):
-                cols = slice(i * width, (i + 1) * width)
-                res = sb("res%d_%d" % (c, i), [P, width], F32)
-                nc.vector.scalar_tensor_tensor(res[:], old_sb[c][:, cols], 0.75, cv[:, cols], MULT, ADD)
-                nc.sync.dma_start(out[c * P : (c + 1) * P, cols], res[:])
+        def finish(c, cv, first, width):
+            cols = slice(first, first + width)
+            res = sb("res%d_%d" % (c, first), [P, width], F32)
+            nc.vector.scalar_tensor_tensor(res[:], old_sb[c][:, cols], 0.75, cv, MULT, ADD)
+            nc.sync.dma_start(out[c * P : (c + 1) * P, cols], res[:])
 
         def quantised(name, values, width):
             codes, scales = sb(name + "_cd", [P, width], U32), sb(name + "_sc", [P, width], U8)
@@ -125,23 +123,24 @@ def tile_picked_crosscov_none_p_kernel(
         raw_a01 = load_cols("raw_a01", wa, 0, HALF, a01_at)
         raw_gate_b = load_gate("raw_gate_b", gi)
         gate_a = load_gate("gate_a", gt)
-        raw_b23 = load_cols("raw_b23", wb, HALF, HALF, b23_at)
         raw_a23 = load_cols("raw_a23", wa, HALF, HALF, a23_at)
+        raw_b2 = load_cols("raw_b2", wb, HALF, CH, b23_at)
+        raw_b3 = load_cols("raw_b3", wb, HALF + CH, CH, b23_at + RAW // 2)
         old_sb = [sb("old%d" % c, [P, H], F32) for c in range(4)]
         for c in range(4):
             nc.sync.dma_start(old_sb[c][:], old[c * P : (c + 1) * P, :])
 
         w_b01, w_a01 = sb("w_b01", [P, HALF, PACK], BF16), sb("w_a01", [P, HALF, PACK], BF16)
-        w_b23 = staged("w_b23", [P, HALF, PACK], BF16, 4 * RAW)
-        w_a2, w_a3 = sb("w_a2", [P, CH, PACK], BF16), sb("w_a3", [P, CH, PACK], BF16)
+        w_a23 = staged("w_a23", [P, HALF, PACK], BF16, 4 * RAW)
+        w_b2, w_b3 = sb("w_b2", [P, CH, PACK], BF16), sb("w_b3", [P, CH, PACK], BF16)
         weave(nc.scalar.copy, w_b01[:, lo, :], raw_b0[:])
         weave(nc.scalar.copy, w_b01[:, hi, :], raw_b1[:])
         weave(nc.scalar.copy, w_a01[:], raw_a01[:])
         gate_b = sb("gate_b", [P, PACK], F32)
         nc.scalar.activation(gate_b[:], raw_gate_b[:], COPY, scale=1.0 / 64)
-        weave(nc.scalar.copy, w_b23[:], raw_b23[:])
-        weave(nc.scalar.copy, w_a2[:], raw_a23[:, :, lo])
-        weave(nc.scalar.copy, w_a3[:], raw_a23[:, :, hi])
+        weave(nc.scalar.copy, w_a23[:], raw_a23[:])
+        weave(nc.scalar.copy, w_b2[:], raw_b2[:])
+        weave(nc.scalar.copy, w_b3[:], raw_b3[:])
 
         xb_sc, xa_sc = sb("xb_sc", [P, S], U8), sb("xa_sc", [P, S], U8)
         xb_cd, xa_cd = sb("xb_cd", [P, S], U32), sb("xa_cd", [P, S], U32)
@@ -153,7 +152,7 @@ def tile_picked_crosscov_none_p_kernel(
 
         z2_lo = staged("z2_lo", [P, HALF, PACK], BF16, a01_at)
         z_0 = staged("z_0", [P, CH, PACK], BF16, b23_at)
-        z2_hi = staged("z2_hi", [P, HALF, PACK], BF16, a23_at)
+        z2_hi = sb("z2_hi", [P, HALF, PACK], BF16)
         z2_cd, z2_sc = sb("z2_cd", [P, H], U32), staged("z2_sc", [P, H], U8, b23_at + RAW // 2)
 
         b0 = project(0, xb_cd, xb_sc, b01_cd[:, lo], b01_sc[:, lo])
@@ -163,20 +162,22 @@ def tile_picked_crosscov_none_p_kernel(
         a0 = project(4, xa_cd, xa_sc, cd[:, lo], sc[:, lo])
         weigh_vector(z2_lo[:, lo, :], b0, gate_b)
         weigh_vector(z2_lo[:, hi, :], b1, gate_b)
-        cd, sc = quantised("b23", w_b23[:], HALF)
-        b2 = project(2, xb_cd, xb_sc, cd[:, lo], sc[:, lo])
-        b3 = project(3, xb_cd, xb_sc, cd[:, hi], sc[:, hi])
-        cd, sc = quantised("a2", w_a2[:], CH)
-        a2 = project(6, xa_cd, xa_sc, cd[:], sc[:])
+        cd, sc = quantised("a23", w_a23[:], HALF)
+        a2 = project(6, xa_cd, xa_sc, cd[:, lo], sc[:, lo])
+        a3 = project(7, xa_cd, xa_sc, cd[:, hi], sc[:, hi])
+        cd, sc = quantised("b2", w_b2[:], CH)
+        b2 = project(2, xb_cd, xb_sc, cd[:], sc[:])
         weigh_vector(z_0[:], a0, gate_a)
-        cd, sc = quantised("a3", w_a3[:], CH)
-        a3 = project(7, xa_cd, xa_sc, cd[:], sc[:])
+        cd, sc = quantised("b3", w_b3[:], CH)
+        b3 = project(3, xb_cd, xb_sc, cd[:], sc[:])
         quantise(z2_cd[:, 0:HALF], z2_sc[:, 0:HALF], z2_lo[:])
 
-        pairs_a1 = staged("pairs_a1", [P, 2, CH, 2], BF16, 4 * RAW)
+        pairs_a1 = staged("pairs_a1", [P, 2, CH, 2], BF16, b23_at + RAW // 4)
         weigh_scalar(pairs_a1, a1, gate_a)
         pairs_a2, pairs_a3 = sb("pairs_a2", [P, 2, CH, 2], BF16), sb("pairs_a3", [P, 2, CH, 2], BF16)
         weigh_scalar(pairs_a2, a2, gate_a)
+        z_1 = sb("z_1", [P, CH, PACK], BF16)
+        join_pairs(nc.scalar.copy, U32, z_1[:], pairs_a1)
         weigh_scalar(pairs_a3, a3, gate_a)
         z_3 = sb("z_3", [P, CH, PACK], BF16)
         join_pairs(nc.scalar.copy, U32, z_3[:], pairs_a3)
@@ -184,31 +185,32 @@ def tile_picked_crosscov_none_p_kernel(
         weigh_vector(z2_hi[:, lo, :], b2, gate_b)
         weigh_vector(z2_hi[:, hi, :], b3, gate_b)
 
-        def moments(i, codes, scales):
-            cv = bank(i, [P, H])
-            product(cv[:], codes[:], scales[:], z2_cd[:], z2_sc[:])
-            return cv
+        def moments(cv, codes, scales, first, width):
+            cols = slice(first, first + width)
+            product(cv, codes[:], scales[:], z2_cd[:, cols], z2_sc[:, cols])
 
-        z0_cd, z0_sc = sb("z0_cd", [P, CH], U32), staged("z0_sc", [P, CH], U8, a23_at + RAW // 2)
+        z0_cd = keep.tile([P, CH], U32, name="z0_cd", tag="z_cd", align_bytes=64)
+        z0_sc = sb("z0_sc", [P, CH], U8)
         quantise(z0_cd[:], z0_sc[:], z_0[:])
-        cv0 = bank(0, [P, H])
-        product(cv0[:, 0:HALF], z0_cd[:], z0_sc[:], z2_cd[:, 0:HALF], z2_sc[:, 0:HALF])
-        z_1 = sb("z_1", [P, CH, PACK], BF16)
-        join_pairs(nc.vector.tensor_copy, F32, z_1[:], pairs_a1)
+        cv0_lo, cv0_hi, cv1 = bank(0, [P, HALF]), bank(4, [P, HALF]), bank(1, [P, H])
+        moments(cv0_lo[:], z0_cd, z0_sc, 0, HALF)
+        z1_cd, z1_sc = quantised("z1", z_1[:], CH)
+        moments(cv1[:, 0:HALF], z1_cd, z1_sc, 0, HALF)
         quantise(z2_cd[:, HALF:H], z2_sc[:, HALF:H], z2_hi[:])
-        product(cv0[:, HALF:H], z0_cd[:], z0_sc[:], z2_cd[:, HALF:H], z2_sc[:, HALF:H])
+        moments(cv0_hi[:], z0_cd, z0_sc, HALF, HALF)
+        moments(cv1[:, HALF:H], z1_cd, z1_sc, HALF, HALF)
         z_2 = sb("z_2", [P, CH, PACK], BF16)
         join_pairs(nc.vector.tensor_copy, F32, z_2[:], pairs_a2)
-        z1_cd = keep.tile([P, CH], U32, name="z1_cd", tag="z_cd", align_bytes=64)
-        z1_sc = sb("z1_sc", [P, CH], U8)
-        quantise(z1_cd[:], z1_sc[:], z_1[:])
-        cv1 = moments(1, z1_cd, z1_sc)
-        cv2 = moments(2, *quantised("z2c", z_2[:], CH))
-        finish(0, cv0, 1)
+        finish(0, cv0_lo[:], 0, HALF)
+        cv2 = bank(2, [P, H])
+        moments(cv2[:], *quantised("z2c", z_2[:], CH), 0, H)
+        finish(0, cv0_hi[:], HALF, HALF)
         z3_cd = keep.tile([P, CH], U32, name="z3_cd", tag="z_cd", align_bytes=64)
         z3_sc = sb("z3_sc", [P, CH], U8)
         quantise(z3_cd[:], z3_sc[:], z_3[:])
-        cv3 = moments(3, z3_cd, z3_sc)
-        finish(1, cv1, 1)
-        finish(2, cv2, 1)
-        finish(3, cv3, 2)
+        cv3 = bank(3, [P, H])
+        moments(cv3[:], z3_cd, z3_sc, 0, H)
+        finish(1, cv1[:], 0, H)
+        finish(2, cv2[:], 0, H)
+        finish(3, cv3[:, 0:HALF], 0, HALF)
+        finish(3, cv3[:, HALF:H], HALF, HALF)

@@ -93,11 +93,13 @@ def tile_picked_crosscov_none_p_kernel(
                 pairs[:].rearrange("p u n e -> p u (n e)").bitcast(word).rearrange("p u n -> p n u"),
             )
 
-        def finish(c, cv, first, width):
-            cols = slice(first, first + width)
-            res = sb("res%d_%d" % (c, first), [P, width], F32)
-            nc.vector.scalar_tensor_tensor(res[:], old_sb[c][:, cols], 0.75, cv, MULT, ADD)
-            nc.sync.dma_start(out[c * P : (c + 1) * P, cols], res[:])
+        def finish(c, cv, pieces):
+            width = H // pieces
+            for i in range(pieces):
+                cols = slice(i * width, (i + 1) * width)
+                res = sb("res%d_%d" % (c, i), [P, width], F32)
+                nc.vector.scalar_tensor_tensor(res[:], old_sb[c][:, cols], 0.75, cv[:, cols], MULT, ADD)
+                nc.sync.dma_start(out[c * P : (c + 1) * P, cols], res[:])
 
         def quantised(name, values, width):
             codes, scales = sb(name + "_cd", [P, width], U32), sb(name + "_sc", [P, width], U8)
@@ -176,8 +178,6 @@ def tile_picked_crosscov_none_p_kernel(
         weigh_scalar(pairs_a1, a1, gate_a)
         pairs_a2, pairs_a3 = sb("pairs_a2", [P, 2, CH, 2], BF16), sb("pairs_a3", [P, 2, CH, 2], BF16)
         weigh_scalar(pairs_a2, a2, gate_a)
-        z_1 = sb("z_1", [P, CH, PACK], BF16)
-        join_pairs(nc.scalar.copy, U32, z_1[:], pairs_a1)
         weigh_scalar(pairs_a3, a3, gate_a)
         z_3 = sb("z_3", [P, CH, PACK], BF16)
         join_pairs(nc.scalar.copy, U32, z_3[:], pairs_a3)
@@ -185,32 +185,31 @@ def tile_picked_crosscov_none_p_kernel(
         weigh_vector(z2_hi[:, lo, :], b2, gate_b)
         weigh_vector(z2_hi[:, hi, :], b3, gate_b)
 
-        def moments(cv, codes, scales, first, width):
-            cols = slice(first, first + width)
-            product(cv, codes[:], scales[:], z2_cd[:, cols], z2_sc[:, cols])
+        def moments(i, codes, scales):
+            cv = bank(i, [P, H])
+            product(cv[:], codes[:], scales[:], z2_cd[:], z2_sc[:])
+            return cv
 
-        z0_cd = keep.tile([P, CH], U32, name="z0_cd", tag="z_cd", align_bytes=64)
-        z0_sc = sb("z0_sc", [P, CH], U8)
+        z0_cd, z0_sc = sb("z0_cd", [P, CH], U32), staged("z0_sc", [P, CH], U8, b23_at + 3 * RAW // 4)
         quantise(z0_cd[:], z0_sc[:], z_0[:])
-        cv0_lo, cv0_hi, cv1 = bank(0, [P, HALF]), bank(4, [P, HALF]), bank(1, [P, H])
-        moments(cv0_lo[:], z0_cd, z0_sc, 0, HALF)
-        z1_cd, z1_sc = quantised("z1", z_1[:], CH)
-        moments(cv1[:, 0:HALF], z1_cd, z1_sc, 0, HALF)
+        cv0 = bank(0, [P, H])
+        product(cv0[:, 0:HALF], z0_cd[:], z0_sc[:], z2_cd[:, 0:HALF], z2_sc[:, 0:HALF])
+        z_1 = sb("z_1", [P, CH, PACK], BF16)
+        join_pairs(nc.vector.tensor_copy, F32, z_1[:], pairs_a1)
         quantise(z2_cd[:, HALF:H], z2_sc[:, HALF:H], z2_hi[:])
-        moments(cv0_hi[:], z0_cd, z0_sc, HALF, HALF)
-        moments(cv1[:, HALF:H], z1_cd, z1_sc, HALF, HALF)
+        product(cv0[:, HALF:H], z0_cd[:], z0_sc[:], z2_cd[:, HALF:H], z2_sc[:, HALF:H])
         z_2 = sb("z_2", [P, CH, PACK], BF16)
         join_pairs(nc.vector.tensor_copy, F32, z_2[:], pairs_a2)
-        finish(0, cv0_lo[:], 0, HALF)
-        cv2 = bank(2, [P, H])
-        moments(cv2[:], *quantised("z2c", z_2[:], CH), 0, H)
-        finish(0, cv0_hi[:], HALF, HALF)
+        z1_cd = keep.tile([P, CH], U32, name="z1_cd", tag="z_cd", align_bytes=64)
+        z1_sc = sb("z1_sc", [P, CH], U8)
+        quantise(z1_cd[:], z1_sc[:], z_1[:])
+        cv1 = moments(1, z1_cd, z1_sc)
+        cv2 = moments(2, *quantised("z2c", z_2[:], CH))
+        finish(0, cv0, 1)
         z3_cd = keep.tile([P, CH], U32, name="z3_cd", tag="z_cd", align_bytes=64)
         z3_sc = sb("z3_sc", [P, CH], U8)
         quantise(z3_cd[:], z3_sc[:], z_3[:])
-        cv3 = bank(3, [P, H])
-        moments(cv3[:], z3_cd, z3_sc, 0, H)
-        finish(1, cv1[:], 0, H)
-        finish(2, cv2[:], 0, H)
-        finish(3, cv3[:, 0:HALF], 0, HALF)
-        finish(3, cv3[:, HALF:H], HALF, HALF)
+        cv3 = moments(3, z3_cd, z3_sc)
+        finish(1, cv1, 1)
+        finish(2, cv2, 1)
+        finish(3, cv3, 2)

@@ -23,6 +23,7 @@ CH = 128
 LINE = 4
 RAW = 4 * PACK * HALF
 PLANE = 4
+EARLY = 512
 
 
 def tile_picked_crosscov_none_p_kernel(
@@ -53,8 +54,11 @@ def tile_picked_crosscov_none_p_kernel(
             nc.sync.dma_start(gate[:], g.rearrange("(p t) o -> p (t o)", t=PACK))
             return gate
 
-        def weave(copy, dst, src):
-            copy(dst.rearrange("p (c i) j -> p c j i", i=LINE), src.rearrange("p j (c i) -> p c j i", i=LINE))
+        def weave(dst, src, factor):
+            nc.scalar.activation(
+                dst.rearrange("p (c i) j -> p c j i", i=LINE), src.rearrange("p j (c i) -> p c j i", i=LINE),
+                COPY, scale=factor,
+            )
 
         def quantise(codes, scales, values):
             nc.vector.quantize_mx(out=codes.bitcast(FP8X4), scales=scales, in_=values.rearrange("p c j -> p (c j)"))
@@ -106,110 +110,96 @@ def tile_picked_crosscov_none_p_kernel(
             quantise(codes[:], scales[:], values)
             return codes, scales
 
-        b0_at, b1_at, a01_at, b23_at, a23_at = 0, RAW // 2, RAW, 2 * RAW, 3 * RAW
+        b01_at, b23_at, a01_at, a23_at = 0, RAW, 2 * RAW, 3 * RAW
         lo, hi = slice(0, CH), slice(CH, HALF)
 
         list_b = keep.tile([P, S // 16], U16, name="list_b")
         list_a = keep.tile([P, S // 16], U16, name="list_a")
         scale_win = sb("scale_win", [P, T], U8)
         word_win = sb("word_win", [P, T], U32)
+        words = x_words[0].rearrange("p n t -> p (n t)").bitcast(I32)
 
         nc.vector.memset(scale_win[:].bitcast(I32), 0)
         nc.sync.dma_start(list_b[:], two)
-        raw_b0 = load_cols("raw_b0", wb, 0, CH, b0_at)
+        nc.sync.dma_start(word_win[:, 0:EARLY].bitcast(I32), words[:, 0:EARLY])
         nc.sync.dma_start(list_a[:], offs)
         for j in range(4):
             nc.sync.dma_start(scale_win[PLANE + j : P : 32, :].bitcast(I32), x_scales[0, j:16:4, :].bitcast(I32))
-        raw_b1 = load_cols("raw_b1", wb, CH, CH, b1_at)
-        nc.sync.dma_start(word_win[:].bitcast(I32), x_words[0].rearrange("p n t -> p (n t)").bitcast(I32))
+        raw_b01 = load_cols("raw_b01", wb, 0, HALF, b01_at)
+        nc.sync.dma_start(word_win[:, EARLY:T].bitcast(I32), words[:, EARLY:T])
+        raw_b23 = load_cols("raw_b23", wb, HALF, HALF, b23_at)
+        gate_b = load_gate("gate_b", gi)
         raw_a01 = load_cols("raw_a01", wa, 0, HALF, a01_at)
-        raw_gate_b = load_gate("raw_gate_b", gi)
-        gate_a = load_gate("gate_a", gt)
         raw_a23 = load_cols("raw_a23", wa, HALF, HALF, a23_at)
-        raw_b2 = load_cols("raw_b2", wb, HALF, CH, b23_at)
-        raw_b3 = load_cols("raw_b3", wb, HALF + CH, CH, b23_at + RAW // 2)
+        gate_a = load_gate("gate_a", gt)
         old_sb = [sb("old%d" % c, [P, H], F32) for c in range(4)]
         for c in range(4):
             nc.sync.dma_start(old_sb[c][:], old[c * P : (c + 1) * P, :])
 
         w_b01, w_a01 = sb("w_b01", [P, HALF, PACK], BF16), sb("w_a01", [P, HALF, PACK], BF16)
-        w_a23 = staged("w_a23", [P, HALF, PACK], BF16, 4 * RAW)
+        w_a23 = sb("w_a23", [P, HALF, PACK], BF16)
         w_b2, w_b3 = sb("w_b2", [P, CH, PACK], BF16), sb("w_b3", [P, CH, PACK], BF16)
-        weave(nc.scalar.copy, w_b01[:, lo, :], raw_b0[:])
-        weave(nc.scalar.copy, w_b01[:, hi, :], raw_b1[:])
-        weave(nc.scalar.copy, w_a01[:], raw_a01[:])
-        gate_b = sb("gate_b", [P, PACK], F32)
-        nc.scalar.activation(gate_b[:], raw_gate_b[:], COPY, scale=1.0 / 64)
-        weave(nc.scalar.copy, w_a23[:], raw_a23[:])
-        weave(nc.scalar.copy, w_b2[:], raw_b2[:])
-        weave(nc.scalar.copy, w_b3[:], raw_b3[:])
+        weave(w_b01[:], raw_b01[:], 1.0 / 64)
+        weave(w_b2[:], raw_b23[:, :, lo], 1.0 / 64)
+        weave(w_b3[:], raw_b23[:, :, hi], 1.0 / 64)
+        weave(w_a01[:], raw_a01[:], 1.0)
+        weave(w_a23[:], raw_a23[:], 1.0)
 
         xb_sc, xa_sc = sb("xb_sc", [P, S], U8), sb("xa_sc", [P, S], U8)
-        xb_cd, xa_cd = sb("xb_cd", [P, S], U32), sb("xa_cd", [P, S], U32)
+        xb_cd, xa_cd = staged("xb_cd", [P, S], U32, b01_at), staged("xa_cd", [P, S], U32, b01_at + RAW // 2)
         pick(xb_sc, scale_win, list_b)
         pick(xa_sc, scale_win, list_a)
         b01_cd, b01_sc = quantised("b01", w_b01[:], HALF)
         pick(xb_cd, word_win, list_b)
         pick(xa_cd, word_win, list_a)
 
-        z2_lo = staged("z2_lo", [P, HALF, PACK], BF16, a01_at)
-        z_0 = staged("z_0", [P, CH, PACK], BF16, b23_at)
-        z2_hi = sb("z2_hi", [P, HALF, PACK], BF16)
-        z2_cd, z2_sc = sb("z2_cd", [P, H], U32), staged("z2_sc", [P, H], U8, b23_at + RAW // 2)
+        z2_lo = staged("z2_lo", [P, HALF, PACK], BF16, b23_at)
+        z2_hi = staged("z2_hi", [P, HALF, PACK], BF16, a01_at)
+        z_0 = staged("z_0", [P, CH, PACK], BF16, a23_at)
+        z2_cd, z2_sc = sb("z2_cd", [P, H], U32), staged("z2_sc", [P, H], U8, a23_at + RAW // 2)
 
         b0 = project(0, xb_cd, xb_sc, b01_cd[:, lo], b01_sc[:, lo])
         b1 = project(1, xb_cd, xb_sc, b01_cd[:, hi], b01_sc[:, hi])
+        cd, sc = quantised("b2", w_b2[:], CH)
+        b2 = project(2, xb_cd, xb_sc, cd[:], sc[:])
+        cd, sc = quantised("b3", w_b3[:], CH)
+        b3 = project(3, xb_cd, xb_sc, cd[:], sc[:])
+        weigh_vector(z2_lo[:, lo, :], b0, gate_b)
+        weigh_vector(z2_lo[:, hi, :], b1, gate_b)
         cd, sc = quantised("a01", w_a01[:], HALF)
         a1 = project(5, xa_cd, xa_sc, cd[:, hi], sc[:, hi])
         a0 = project(4, xa_cd, xa_sc, cd[:, lo], sc[:, lo])
-        weigh_vector(z2_lo[:, lo, :], b0, gate_b)
-        weigh_vector(z2_lo[:, hi, :], b1, gate_b)
+        weigh_vector(z2_hi[:, lo, :], b2, gate_b)
+        weigh_vector(z2_hi[:, hi, :], b3, gate_b)
         cd, sc = quantised("a23", w_a23[:], HALF)
         a2 = project(6, xa_cd, xa_sc, cd[:, lo], sc[:, lo])
         a3 = project(7, xa_cd, xa_sc, cd[:, hi], sc[:, hi])
-        cd, sc = quantised("b2", w_b2[:], CH)
-        b2 = project(2, xb_cd, xb_sc, cd[:], sc[:])
         weigh_vector(z_0[:], a0, gate_a)
-        cd, sc = quantised("b3", w_b3[:], CH)
-        b3 = project(3, xb_cd, xb_sc, cd[:], sc[:])
-        quantise(z2_cd[:, 0:HALF], z2_sc[:, 0:HALF], z2_lo[:])
 
-        pairs_a1 = staged("pairs_a1", [P, 2, CH, 2], BF16, b23_at + RAW // 4)
+        pairs_a1, pairs_a2 = sb("pairs_a1", [P, 2, CH, 2], BF16), sb("pairs_a2", [P, 2, CH, 2], BF16)
+        pairs_a3 = sb("pairs_a3", [P, 2, CH, 2], BF16)
         weigh_scalar(pairs_a1, a1, gate_a)
-        pairs_a2, pairs_a3 = sb("pairs_a2", [P, 2, CH, 2], BF16), sb("pairs_a3", [P, 2, CH, 2], BF16)
         weigh_scalar(pairs_a2, a2, gate_a)
         weigh_scalar(pairs_a3, a3, gate_a)
         z_3 = sb("z_3", [P, CH, PACK], BF16)
         join_pairs(nc.scalar.copy, U32, z_3[:], pairs_a3)
 
-        weigh_vector(z2_hi[:, lo, :], b2, gate_b)
-        weigh_vector(z2_hi[:, hi, :], b3, gate_b)
+        quantise(z2_cd[:, 0:HALF], z2_sc[:, 0:HALF], z2_lo[:])
+        quantise(z2_cd[:, HALF:H], z2_sc[:, HALF:H], z2_hi[:])
 
         def moments(i, codes, scales):
             cv = bank(i, [P, H])
             product(cv[:], codes[:], scales[:], z2_cd[:], z2_sc[:])
             return cv
 
-        z0_cd, z0_sc = sb("z0_cd", [P, CH], U32), staged("z0_sc", [P, CH], U8, b23_at + 3 * RAW // 4)
-        quantise(z0_cd[:], z0_sc[:], z_0[:])
-        cv0 = bank(0, [P, H])
-        product(cv0[:, 0:HALF], z0_cd[:], z0_sc[:], z2_cd[:, 0:HALF], z2_sc[:, 0:HALF])
-        z_1 = sb("z_1", [P, CH, PACK], BF16)
+        cv0 = moments(0, *quantised("z0", z_0[:], CH))
+        z_1, z_2 = sb("z_1", [P, CH, PACK], BF16), sb("z_2", [P, CH, PACK], BF16)
         join_pairs(nc.vector.tensor_copy, F32, z_1[:], pairs_a1)
-        quantise(z2_cd[:, HALF:H], z2_sc[:, HALF:H], z2_hi[:])
-        product(cv0[:, HALF:H], z0_cd[:], z0_sc[:], z2_cd[:, HALF:H], z2_sc[:, HALF:H])
-        z_2 = sb("z_2", [P, CH, PACK], BF16)
         join_pairs(nc.vector.tensor_copy, F32, z_2[:], pairs_a2)
-        z1_cd = keep.tile([P, CH], U32, name="z1_cd", tag="z_cd", align_bytes=64)
-        z1_sc = sb("z1_sc", [P, CH], U8)
-        quantise(z1_cd[:], z1_sc[:], z_1[:])
-        cv1 = moments(1, z1_cd, z1_sc)
+        cv1 = moments(1, *quantised("z1", z_1[:], CH))
         cv2 = moments(2, *quantised("z2c", z_2[:], CH))
         finish(0, cv0, 1)
-        z3_cd = keep.tile([P, CH], U32, name="z3_cd", tag="z_cd", align_bytes=64)
-        z3_sc = sb("z3_sc", [P, CH], U8)
-        quantise(z3_cd[:], z3_sc[:], z_3[:])
-        cv3 = moments(3, z3_cd, z3_sc)
         finish(1, cv1, 1)
+        cv3 = moments(3, *quantised("z3", z_3[:], CH))
         finish(2, cv2, 1)
         finish(3, cv3, 2)

@@ -23,7 +23,6 @@ CH = 128
 LINE = 4
 RAW = 4 * PACK * HALF
 PLANE = 4
-EARLY = 512
 
 
 def tile_picked_crosscov_none_p_kernel(
@@ -121,12 +120,12 @@ def tile_picked_crosscov_none_p_kernel(
 
         nc.vector.memset(scale_win[:].bitcast(I32), 0)
         nc.sync.dma_start(list_b[:], two)
-        nc.sync.dma_start(word_win[:, 0:EARLY].bitcast(I32), words[:, 0:EARLY])
+        raw_b0 = load_cols("raw_b0", wb, 0, CH, b01_at)
         nc.sync.dma_start(list_a[:], offs)
         for j in range(4):
             nc.sync.dma_start(scale_win[PLANE + j : P : 32, :].bitcast(I32), x_scales[0, j:16:4, :].bitcast(I32))
-        raw_b01 = load_cols("raw_b01", wb, 0, HALF, b01_at)
-        nc.sync.dma_start(word_win[:, EARLY:T].bitcast(I32), words[:, EARLY:T])
+        raw_b1 = load_cols("raw_b1", wb, CH, CH, b01_at + RAW // 2)
+        nc.sync.dma_start(word_win[:].bitcast(I32), words)
         raw_b23 = load_cols("raw_b23", wb, HALF, HALF, b23_at)
         gate_b = load_gate("gate_b", gi)
         raw_a01 = load_cols("raw_a01", wa, 0, HALF, a01_at)
@@ -139,14 +138,15 @@ def tile_picked_crosscov_none_p_kernel(
         w_b01, w_a01 = sb("w_b01", [P, HALF, PACK], BF16), sb("w_a01", [P, HALF, PACK], BF16)
         w_a23 = sb("w_a23", [P, HALF, PACK], BF16)
         w_b2, w_b3 = sb("w_b2", [P, CH, PACK], BF16), sb("w_b3", [P, CH, PACK], BF16)
-        weave(w_b01[:], raw_b01[:], 1.0 / 64)
+        weave(w_b01[:, lo, :], raw_b0[:], 1.0 / 64)
+        weave(w_b01[:, hi, :], raw_b1[:], 1.0 / 64)
         weave(w_b2[:], raw_b23[:, :, lo], 1.0 / 64)
         weave(w_b3[:], raw_b23[:, :, hi], 1.0 / 64)
         weave(w_a01[:], raw_a01[:], 1.0)
         weave(w_a23[:], raw_a23[:], 1.0)
 
         xb_sc, xa_sc = sb("xb_sc", [P, S], U8), sb("xa_sc", [P, S], U8)
-        xb_cd, xa_cd = staged("xb_cd", [P, S], U32, b01_at), staged("xa_cd", [P, S], U32, b01_at + RAW // 2)
+        xb_cd, xa_cd = sb("xb_cd", [P, S], U32), sb("xa_cd", [P, S], U32)
         pick(xb_sc, scale_win, list_b)
         pick(xa_sc, scale_win, list_a)
         b01_cd, b01_sc = quantised("b01", w_b01[:], HALF)
@@ -155,8 +155,7 @@ def tile_picked_crosscov_none_p_kernel(
 
         z2_lo = staged("z2_lo", [P, HALF, PACK], BF16, b23_at)
         z2_hi = staged("z2_hi", [P, HALF, PACK], BF16, a01_at)
-        z_0 = staged("z_0", [P, CH, PACK], BF16, a23_at)
-        z2_cd, z2_sc = sb("z2_cd", [P, H], U32), staged("z2_sc", [P, H], U8, a23_at + RAW // 2)
+        z2_cd, z2_sc = sb("z2_cd", [P, H], U32), staged("z2_sc", [P, H], U8, a23_at)
 
         b0 = project(0, xb_cd, xb_sc, b01_cd[:, lo], b01_sc[:, lo])
         b1 = project(1, xb_cd, xb_sc, b01_cd[:, hi], b01_sc[:, hi])
@@ -167,19 +166,18 @@ def tile_picked_crosscov_none_p_kernel(
         weigh_vector(z2_lo[:, lo, :], b0, gate_b)
         weigh_vector(z2_lo[:, hi, :], b1, gate_b)
         cd, sc = quantised("a01", w_a01[:], HALF)
-        a1 = project(5, xa_cd, xa_sc, cd[:, hi], sc[:, hi])
         a0 = project(4, xa_cd, xa_sc, cd[:, lo], sc[:, lo])
+        a1 = project(5, xa_cd, xa_sc, cd[:, hi], sc[:, hi])
         weigh_vector(z2_hi[:, lo, :], b2, gate_b)
         weigh_vector(z2_hi[:, hi, :], b3, gate_b)
         cd, sc = quantised("a23", w_a23[:], HALF)
         a2 = project(6, xa_cd, xa_sc, cd[:, lo], sc[:, lo])
         a3 = project(7, xa_cd, xa_sc, cd[:, hi], sc[:, hi])
-        weigh_vector(z_0[:], a0, gate_a)
 
-        pairs_a1, pairs_a2 = sb("pairs_a1", [P, 2, CH, 2], BF16), sb("pairs_a2", [P, 2, CH, 2], BF16)
+        pairs_a0, pairs_a1 = sb("pairs_a0", [P, 2, CH, 2], BF16), sb("pairs_a1", [P, 2, CH, 2], BF16)
         pairs_a3 = sb("pairs_a3", [P, 2, CH, 2], BF16)
+        weigh_scalar(pairs_a0, a0, gate_a)
         weigh_scalar(pairs_a1, a1, gate_a)
-        weigh_scalar(pairs_a2, a2, gate_a)
         weigh_scalar(pairs_a3, a3, gate_a)
         z_3 = sb("z_3", [P, CH, PACK], BF16)
         join_pairs(nc.scalar.copy, U32, z_3[:], pairs_a3)
@@ -192,14 +190,15 @@ def tile_picked_crosscov_none_p_kernel(
             product(cv[:], codes[:], scales[:], z2_cd[:], z2_sc[:])
             return cv
 
+        z_0, z_1, z_2 = (sb("z_%d" % c, [P, CH, PACK], BF16) for c in range(3))
+        join_pairs(nc.vector.tensor_copy, F32, z_0[:], pairs_a0)
+        weigh_vector(z_2[:], a2, gate_a)
         cv0 = moments(0, *quantised("z0", z_0[:], CH))
-        z_1, z_2 = sb("z_1", [P, CH, PACK], BF16), sb("z_2", [P, CH, PACK], BF16)
-        join_pairs(nc.vector.tensor_copy, F32, z_1[:], pairs_a1)
-        join_pairs(nc.vector.tensor_copy, F32, z_2[:], pairs_a2)
-        cv1 = moments(1, *quantised("z1", z_1[:], CH))
         cv2 = moments(2, *quantised("z2c", z_2[:], CH))
+        join_pairs(nc.vector.tensor_copy, F32, z_1[:], pairs_a1)
         finish(0, cv0, 1)
-        finish(1, cv1, 1)
-        cv3 = moments(3, *quantised("z3", z_3[:], CH))
+        cv1 = moments(1, *quantised("z1", z_1[:], CH))
         finish(2, cv2, 1)
+        cv3 = moments(3, *quantised("z3", z_3[:], CH))
+        finish(1, cv1, 1)
         finish(3, cv3, 2)

@@ -35,10 +35,10 @@ def tile_picked_crosscov_none_p_kernel(
         psum = ctx.enter_context(tc.psum_pool(name="psum", bufs=1))
 
         def sb(name, shape, dtype):
-            return keep.tile(shape, dtype, name=name, align_bytes=64)
+            return keep.tile(shape, dtype, name=name, align_bytes=256)
 
         def staged(name, shape, dtype, offset):
-            return stage.tile(shape, dtype, name=name, offset=offset, align_bytes=64)
+            return stage.tile(shape, dtype, name=name, offset=offset, align_bytes=256)
 
         def bank(i, shape):
             return psum.tile(shape, F32, name="bank", tag="bank%d" % i)
@@ -53,11 +53,8 @@ def tile_picked_crosscov_none_p_kernel(
             nc.sync.dma_start(gate[:], g.rearrange("(p t) o -> p (t o)", t=PACK))
             return gate
 
-        def weave(dst, src, factor):
-            nc.scalar.activation(
-                dst.rearrange("p (c i) j -> p c j i", i=LINE), src.rearrange("p j (c i) -> p c j i", i=LINE),
-                COPY, scale=factor,
-            )
+        def weave(copy, dst, src):
+            copy(dst.rearrange("p (c i) j -> p c j i", i=LINE), src.rearrange("p j (c i) -> p c j i", i=LINE))
 
         def quantise(codes, scales, values):
             nc.vector.quantize_mx(out=codes.bitcast(FP8X4), scales=scales, in_=values.rearrange("p c j -> p (c j)"))
@@ -127,7 +124,7 @@ def tile_picked_crosscov_none_p_kernel(
         raw_b1 = load_cols("raw_b1", wb, CH, CH, b01_at + RAW // 2)
         nc.sync.dma_start(word_win[:].bitcast(I32), words)
         raw_b23 = load_cols("raw_b23", wb, HALF, HALF, b23_at)
-        gate_b = load_gate("gate_b", gi)
+        raw_gate_b = load_gate("raw_gate_b", gi)
         raw_a01 = load_cols("raw_a01", wa, 0, HALF, a01_at)
         raw_a23 = load_cols("raw_a23", wa, HALF, HALF, a23_at)
         gate_a = load_gate("gate_a", gt)
@@ -138,12 +135,14 @@ def tile_picked_crosscov_none_p_kernel(
         w_b01, w_a01 = sb("w_b01", [P, HALF, PACK], BF16), sb("w_a01", [P, HALF, PACK], BF16)
         w_a23 = sb("w_a23", [P, HALF, PACK], BF16)
         w_b2, w_b3 = sb("w_b2", [P, CH, PACK], BF16), sb("w_b3", [P, CH, PACK], BF16)
-        weave(w_b01[:, lo, :], raw_b0[:], 1.0 / 64)
-        weave(w_b01[:, hi, :], raw_b1[:], 1.0 / 64)
-        weave(w_b2[:], raw_b23[:, :, lo], 1.0 / 64)
-        weave(w_b3[:], raw_b23[:, :, hi], 1.0 / 64)
-        weave(w_a01[:], raw_a01[:], 1.0)
-        weave(w_a23[:], raw_a23[:], 1.0)
+        weave(nc.scalar.copy, w_b01[:, lo, :], raw_b0[:])
+        weave(nc.scalar.copy, w_b01[:, hi, :], raw_b1[:])
+        weave(nc.scalar.copy, w_b2[:], raw_b23[:, :, lo])
+        weave(nc.scalar.copy, w_b3[:], raw_b23[:, :, hi])
+        gate_b = sb("gate_b", [P, PACK], F32)
+        nc.scalar.activation(gate_b[:], raw_gate_b[:], COPY, scale=1.0 / 64)
+        weave(nc.scalar.copy, w_a01[:], raw_a01[:])
+        weave(nc.scalar.copy, w_a23[:], raw_a23[:])
 
         xb_sc, xa_sc = sb("xb_sc", [P, S], U8), sb("xa_sc", [P, S], U8)
         xb_cd, xa_cd = sb("xb_cd", [P, S], U32), sb("xa_cd", [P, S], U32)

@@ -117,11 +117,13 @@ def tile_picked_crosscov_none_p_kernel(
 
         nc.vector.memset(scale_win[:].bitcast(I32), 0)
         nc.sync.dma_start(list_b[:], two)
-        raw_b0 = load_cols("raw_b0", wb, 0, CH, b01_at)
+        raw_b01 = staged("raw_b01", [P, PACK, HALF], F32, b01_at)
+        wb_lo = wb.rearrange("(p j) c -> p j c", j=PACK)[:, :, 0:HALF]
+        nc.sync.dma_start(raw_b01[:, 0:2, :], wb_lo[:, 0:2, :])
         nc.sync.dma_start(list_a[:], offs)
         for j in range(4):
             nc.sync.dma_start(scale_win[PLANE + j : P : 32, :].bitcast(I32), x_scales[0, j:16:4, :].bitcast(I32))
-        raw_b1 = load_cols("raw_b1", wb, CH, CH, b01_at + RAW // 2)
+        nc.sync.dma_start(raw_b01[:, 2:4, :], wb_lo[:, 2:4, :])
         nc.sync.dma_start(word_win[:].bitcast(I32), words)
         raw_b23 = load_cols("raw_b23", wb, HALF, HALF, b23_at)
         raw_gate_b = load_gate("raw_gate_b", gi)
@@ -135,8 +137,8 @@ def tile_picked_crosscov_none_p_kernel(
         w_b01, w_a01 = sb("w_b01", [P, HALF, PACK], BF16), sb("w_a01", [P, HALF, PACK], BF16)
         w_a23 = sb("w_a23", [P, HALF, PACK], BF16)
         w_b2, w_b3 = sb("w_b2", [P, CH, PACK], BF16), sb("w_b3", [P, CH, PACK], BF16)
-        weave(nc.scalar.copy, w_b01[:, lo, :], raw_b0[:])
-        weave(nc.scalar.copy, w_b01[:, hi, :], raw_b1[:])
+        weave(nc.scalar.copy, w_b01[:, :, 0:2], raw_b01[:, 0:2, :])
+        weave(nc.scalar.copy, w_b01[:, :, 2:4], raw_b01[:, 2:4, :])
         weave(nc.scalar.copy, w_b2[:], raw_b23[:, :, lo])
         weave(nc.scalar.copy, w_b3[:], raw_b23[:, :, hi])
         gate_b = sb("gate_b", [P, PACK], F32)
@@ -145,7 +147,7 @@ def tile_picked_crosscov_none_p_kernel(
         weave(nc.scalar.copy, w_a23[:], raw_a23[:])
 
         xb_sc, xa_sc = sb("xb_sc", [P, S], U8), sb("xa_sc", [P, S], U8)
-        xb_cd, xa_cd = sb("xb_cd", [P, S], U32), sb("xa_cd", [P, S], U32)
+        xb_cd, xa_cd = staged("xb_cd", [P, S], U32, b01_at), staged("xa_cd", [P, S], U32, b01_at + RAW // 2)
         pick(xb_sc, scale_win, list_b)
         pick(xa_sc, scale_win, list_a)
         b01_cd, b01_sc = quantised("b01", w_b01[:], HALF)
@@ -199,5 +201,5 @@ def tile_picked_crosscov_none_p_kernel(
         cv1 = moments(1, *quantised("z1", z_1[:], CH))
         finish(2, cv2, 1)
         cv3 = moments(3, *quantised("z3", z_3[:], CH))
-        finish(1, cv1, 1)
+        finish(1, cv1, 2)
         finish(3, cv3, 2)

@@ -98,7 +98,7 @@ def tile_picked_crosscov_none_p_kernel(
             for i in range(pieces):
                 cols = slice(i * width, (i + 1) * width)
                 res = sb("res%d_%d" % (c, i), [P, width], F32)
-                nc.vector.scalar_tensor_tensor(res[:], old_sb[c][:, cols], 0.75, cv[:, cols], MULT, ADD)
+                nc.vector.scalar_tensor_tensor(res[:], old_pairs[c % 2][:, c // 2, cols], 0.75, cv[:, cols], MULT, ADD)
                 nc.sync.dma_start(out[c * P : (c + 1) * P, cols], res[:])
 
         def quantised(name, values, width):
@@ -130,9 +130,9 @@ def tile_picked_crosscov_none_p_kernel(
         raw_a01 = load_cols("raw_a01", wa, 0, HALF, a01_at)
         raw_a23 = load_cols("raw_a23", wa, HALF, HALF, a23_at)
         gate_a = load_gate("gate_a", gt)
-        old_sb = [sb("old%d" % c, [P, H], F32) for c in range(4)]
-        for c in range(4):
-            nc.sync.dma_start(old_sb[c][:], old[c * P : (c + 1) * P, :])
+        old_pairs = [sb("old%d" % c, [P, 2, H], F32) for c in range(2)]
+        for c in range(2):
+            nc.sync.dma_start(old_pairs[c][:], old.rearrange("(h c p) n -> c p h n", h=2, c=2)[c])
 
         w_b01, w_a01 = sb("w_b01", [P, HALF, PACK], BF16), sb("w_a01", [P, HALF, PACK], BF16)
         w_a23 = sb("w_a23", [P, HALF, PACK], BF16)
@@ -197,9 +197,9 @@ def tile_picked_crosscov_none_p_kernel(
         cv0 = moments(0, *quantised("z0", z_0[:], CH))
         cv2 = moments(2, *quantised("z2c", z_2[:], CH))
         join_pairs(nc.vector.tensor_copy, F32, z_1[:], pairs_a1)
-        finish(0, cv0, 1)
+        finish(0, cv0, 2)
         cv1 = moments(1, *quantised("z1", z_1[:], CH))
-        finish(2, cv2, 1)
+        finish(2, cv2, 2)
         cv3 = moments(3, *quantised("z3", z_3[:], CH))
         finish(1, cv1, 2)
         finish(3, cv3, 2)

from contextlib import ExitStack

import concourse.mybir as mybir

K, T, S, H = 512, 2048, 512, 512
FLOPS = 3 * 2 * 512 * 512 * 512

F32 = mybir.dt.float32
BF16 = mybir.dt.bfloat16
I32 = mybir.dt.int32
U32 = mybir.dt.uint32
U16 = mybir.dt.uint16
U8 = mybir.dt.uint8
FP8X4 = mybir.dt.float8_e4m3fn_x4
MULT = mybir.AluOpType.mult
ADD = mybir.AluOpType.add
COPY = mybir.ActivationFunctionType.Copy

P = 128
PACK = 4
HALF = H // 2
CH = 128
LINE = 4
RAW = 4 * PACK * HALF
PLANE = 4


def tile_picked_crosscov_none_p_kernel(
    tc, x_words, x_scales, wa, wb, gt, gi, old, offs, two, out
):
    nc = tc.nc
    with ExitStack() as ctx:
        keep = ctx.enter_context(tc.tile_pool(name="keep", bufs=1))
        stage = ctx.enter_context(tc.tile_pool(name="stage", bufs=1))
        psum = ctx.enter_context(tc.psum_pool(name="psum", bufs=1))

        def sb(name, shape, dtype):
            return keep.tile(shape, dtype, name=name, align_bytes=256)

        def staged(name, shape, dtype, offset):
            return stage.tile(shape, dtype, name=name, offset=offset, align_bytes=256)

        def bank(i, shape):
            return psum.tile(shape, F32, name="bank", tag="bank%d" % i)

        def load_cols(name, w, first, width, offset):
            raw = staged(name, [P, PACK, width], F32, offset)
            nc.sync.dma_start(raw[:], w.rearrange("(p j) c -> p j c", j=PACK)[:, :, first : first + width])
            return raw

        def load_gate(name, g):
            gate = sb(name, [P, PACK], F32)
            nc.sync.dma_start(gate[:], g.rearrange("(p t) o -> p (t o)", t=PACK))
            return gate

        def weave(copy, dst, src):
            copy(dst.rearrange("p (c i) j -> p c j i", i=LINE), src.rearrange("p j (c i) -> p c j i", i=LINE))

        def quantise(codes, scales, values):
            nc.vector.quantize_mx(out=codes.bitcast(FP8X4), scales=scales, in_=values.rearrange("p c j -> p (c j)"))

        def product(dst, lhs, lhs_sc, rhs, rhs_sc):
            nc.tensor.matmul_mx(
                out=dst, lhsT=lhs.bitcast(FP8X4), lhsT_scale=lhs_sc, rhs=rhs.bitcast(FP8X4), rhs_scale=rhs_sc,
                start=True, stop=True,
            )

        def pick(dst, window, places):
            nc.vector.tensor_copy(dst[:].rearrange("p (t m) -> p m t", t=PACK), window[:].indirect(places[:]))

        def project(i, x_cd, x_sc, w_cd, w_sc):
            dst = bank(i, [P, PACK, CH])
            for t in range(PACK):
                rows = slice(t * P, (t + 1) * P)
                product(dst[:, t, :], x_cd[:, rows], x_sc[PLANE:P, rows], w_cd, w_sc)
            return dst

        def weigh_vector(dst, src, gate):
            nc.vector.tensor_tensor(
                dst,
                src[:].rearrange("p t n -> p n t"),
                gate[:].rearrange("p (o t) -> p o t", o=1).to_broadcast([P, CH, PACK]),
                MULT,
            )

        def weigh_scalar(pairs, src, gate):
            for t in range(PACK):
                nc.scalar.activation(pairs[:, t // 2, :, t % 2], src[:, t, :], COPY, scale=gate[:, t : t + 1])

        def join_pairs(copy, word, dst, pairs):
            copy(
                dst.bitcast(word),
                pairs[:].rearrange("p u n e -> p u (n e)").bitcast(word).rearrange("p u n -> p n u"),
            )

        def finish(c, cv, pieces):
            width = H // pieces
            for i in range(pieces):
                cols = slice(i * width, (i + 1) * width)
                res = sb("res%d_%d" % (c, i), [P, width], F32)
                nc.vector.scalar_tensor_tensor(res[:], old_pairs[c % 2][:, c // 2, cols], 0.75, cv[:, cols], MULT, ADD)
                nc.sync.dma_start(out[c * P : (c + 1) * P, cols], res[:])

        def quantised(name, values, width):
            codes, scales = sb(name + "_cd", [P, width], U32), sb(name + "_sc", [P, width], U8)
            quantise(codes[:], scales[:], values)
            return codes, scales

        b01_at, b23_at, a01_at, a23_at = 0, RAW, 2 * RAW, 3 * RAW
        lo, hi = slice(0, CH), slice(CH, HALF)

        list_b = keep.tile([P, S // 16], U16, name="list_b")
        list_a = keep.tile([P, S // 16], U16, name="list_a")
        scale_win = sb("scale_win", [P, T], U8)
        word_win = sb("word_win", [P, T], U32)
        words = x_words[0].rearrange("p n t -> p (n t)").bitcast(I32)

        nc.vector.memset(scale_win[:].bitcast(I32), 0)
        nc.sync.dma_start(list_b[:], two)
        raw_b01 = staged("raw_b01", [P, PACK, HALF], F32, b01_at)
        wb_lo = wb.rearrange("(p j) c -> p j c", j=PACK)[:, :, 0:HALF]
        nc.sync.dma_start(raw_b01[:, 0:2, :], wb_lo[:, 0:2, :])
        nc.sync.dma_start(list_a[:], offs)
        for j in range(4):
            nc.sync.dma_start(scale_win[PLANE + j : P : 32, :].bitcast(I32), x_scales[0, j:16:4, :].bitcast(I32))
        nc.sync.dma_start(raw_b01[:, 2:4, :], wb_lo[:, 2:4, :])
        nc.sync.dma_start(word_win[:].bitcast(I32), words)
        raw_b23 = load_cols("raw_b23", wb, HALF, HALF, b23_at)
        raw_gate_b = load_gate("raw_gate_b", gi)
        raw_a01 = load_cols("raw_a01", wa, 0, HALF, a01_at)
        raw_a23 = load_cols("raw_a23", wa, HALF, HALF, a23_at)
        gate_a = load_gate("gate_a", gt)
        old_pairs = [sb("old%d" % c, [P, 2, H], F32) for c in range(2)]
        for c in range(2):
            nc.sync.dma_start(old_pairs[c][:], old.rearrange("(h c p) n -> c p h n", h=2, c=2)[c])

        w_b01, w_a01 = sb("w_b01", [P, HALF, PACK], BF16), sb("w_a01", [P, HALF, PACK], BF16)
        w_a23 = sb("w_a23", [P, HALF, PACK], BF16)
        w_b2, w_b3 = sb("w_b2", [P, CH, PACK], BF16), sb("w_b3", [P, CH, PACK], BF16)
        weave(nc.scalar.copy, w_b01[:, :, 0:2], raw_b01[:, 0:2, :])
        weave(nc.scalar.copy, w_b01[:, :, 2:4], raw_b01[:, 2:4, :])
        weave(nc.scalar.copy, w_b2[:], raw_b23[:, :, lo])
        weave(nc.scalar.copy, w_b3[:], raw_b23[:, :, hi])
        gate_b = sb("gate_b", [P, PACK], F32)
        nc.scalar.activation(gate_b[:], raw_gate_b[:], COPY, scale=1.0 / 64)
        weave(nc.scalar.copy, w_a01[:], raw_a01[:])
        weave(nc.scalar.copy, w_a23[:], raw_a23[:])

        xb_sc, xa_sc = sb("xb_sc", [P, S], U8), sb("xa_sc", [P, S], U8)
        xb_cd, xa_cd = staged("xb_cd", [P, S], U32, b01_at), staged("xa_cd", [P, S], U32, b01_at + RAW // 2)
        pick(xb_sc, scale_win, list_b)
        pick(xa_sc, scale_win, list_a)
        b01_cd, b01_sc = quantised("b01", w_b01[:], HALF)
        pick(xb_cd, word_win, list_b)
        pick(xa_cd, word_win, list_a)

        z2_lo = staged("z2_lo", [P, HALF, PACK], BF16, b23_at)
        z2_hi = staged("z2_hi", [P, HALF, PACK], BF16, a01_at)
        z2_cd, z2_sc = sb("z2_cd", [P, H], U32), staged("z2_sc", [P, H], U8, a23_at)

        b0 = project(0, xb_cd, xb_sc, b01_cd[:, lo], b01_sc[:, lo])
        b1 = project(1, xb_cd, xb_sc, b01_cd[:, hi], b01_sc[:, hi])
        cd, sc = quantised("b2", w_b2[:], CH)
        b2 = project(2, xb_cd, xb_sc, cd[:], sc[:])
        cd, sc = quantised("b3", w_b3[:], CH)
        b3 = project(3, xb_cd, xb_sc, cd[:], sc[:])
        weigh_vector(z2_lo[:, lo, :], b0, gate_b)
        weigh_vector(z2_lo[:, hi, :], b1, gate_b)
        cd, sc = quantised("a01", w_a01[:], HALF)
        a0 = project(4, xa_cd, xa_sc, cd[:, lo], sc[:, lo])
        a1 = project(5, xa_cd, xa_sc, cd[:, hi], sc[:, hi])
        weigh_vector(z2_hi[:, lo, :], b2, gate_b)
        weigh_vector(z2_hi[:, hi, :], b3, gate_b)
        cd, sc = quantised("a23", w_a23[:], HALF)
        a2 = project(6, xa_cd, xa_sc, cd[:, lo], sc[:, lo])
        a3 = project(7, xa_cd, xa_sc, cd[:, hi], sc[:, hi])

        pairs_a0, pairs_a1 = sb("pairs_a0", [P, 2, CH, 2], BF16), sb("pairs_a1", [P, 2, CH, 2], BF16)
        pairs_a3 = sb("pairs_a3", [P, 2, CH, 2], BF16)
        weigh_scalar(pairs_a0, a0, gate_a)
        weigh_scalar(pairs_a1, a1, gate_a)
        weigh_scalar(pairs_a3, a3, gate_a)
        z_3 = sb("z_3", [P, CH, PACK], BF16)
        join_pairs(nc.scalar.copy, U32, z_3[:], pairs_a3)

        quantise(z2_cd[:, 0:HALF], z2_sc[:, 0:HALF], z2_lo[:])
        quantise(z2_cd[:, HALF:H], z2_sc[:, HALF:H], z2_hi[:])

        def moments(i, codes, scales):
            cv = bank(i, [P, H])
            product(cv[:], codes[:], scales[:], z2_cd[:], z2_sc[:])
            return cv

        z_0, z_1, z_2 = (sb("z_%d" % c, [P, CH, PACK], BF16) for c in range(3))
        join_pairs(nc.vector.tensor_copy, F32, z_0[:], pairs_a0)
        weigh_vector(z_2[:], a2, gate_a)
        cv0 = moments(0, *quantised("z0", z_0[:], CH))
        cv2 = moments(2, *quantised("z2c", z_2[:], CH))
        join_pairs(nc.vector.tensor_copy, F32, z_1[:], pairs_a1)
        finish(0, cv0, 2)
        cv1 = moments(1, *quantised("z1", z_1[:], CH))
        finish(2, cv2, 2)
        cv3 = moments(3, *quantised("z3", z_3[:], CH))
        finish(1, cv1, 2)
        finish(3, cv3, 2)
